import numpy as np, ml_dtypes
CORES = [16,18,20,22]
N = 4
BF = ml_dtypes.bfloat16
def gentries(a):
    return np.ascontiguousarray(a.reshape(8, 16, -1).transpose(0, 2, 1)).reshape(8, -1)
def gtable(e):
    e = np.asarray(e); return np.ascontiguousarray(e.reshape(8, -1, 16).transpose(0, 2, 1)).reshape(128, -1).astype(np.int32)
V, U, S, C, RO = 512, 512, 8, 1, 4
X, M, NONE = V + U, N * V, N * V + U
def cut(p, c):
    return np.where(np.arange(S) < c[..., None], p, NONE)
def around(rng, o, j):
    j = np.minimum(j, o); m = np.maximum(S - 1 - j, 1)
    below = rng.integers(1, np.maximum(o // np.maximum(j, 1), 1) + 1); above = rng.integers(1, np.maximum((M - 1 - o) // m, 1) + 1)
    d = np.arange(S) - j[..., None]; x = o[..., None] + np.where(d < 0, below[..., None], above[..., None]) * d
    return np.where(x < M, x, NONE)
def hold(rng, o, lo, hi):
    n = hi - lo; d = np.sort(rng.integers(0, n - S + 1, o.shape + (S - 1,)), axis=-1) + np.arange(1, S)
    d = np.concatenate([np.zeros(o.shape + (1,), np.int64), d], axis=-1)
    return np.sort(lo + (o[..., None] - lo + d) % n, axis=-1)
def numbers_of():
    return np.arange(M).reshape(N, 1, V) + np.zeros((1, 8, 1), np.int64)
def parts(rng):
    size = rng.random((N, 8, X, 1)); low = rng.random((N, 8, X, 1)) * (1 - size)
    x = np.minimum((low + size * rng.random((N, 8, X, S))) * (M - S + 1), M - S).astype(np.int64)
    p = cut(np.sort(x, axis=-1) + np.arange(S), rng.integers(0, S + 1, (N, 8, X)))
    return p, rng.integers(0, NONE + 1, (N, 8, X)), rng.integers(0, NONE + 1, (N, 8, C, X)), rng.integers(0, NONE + 1, (N, 8, V)), rng.integers(0, NONE + 1, (N, 8, V))
def name(rng, p, xs):
    xs = np.array(xs)
    for r in range(N):
        for g in range(8):
            tab = np.concatenate([p[:, g, :V].reshape(M, S), p[r, g, V:]])
            place, slot = np.nonzero(tab // V == r); k = rng.permutation(len(place))
            new = np.array(xs[r, g]); new[tab[place[k], slot[k]] - r * V] = place[k]
            xs[r, g] = np.where(rng.random(V) < 0.65, new, xs[r, g])
    return xs
def pack(p, ld, cp, xs, ys):
    a = np.full((N, 8, 16, X), NONE, np.int32); a[:, :, :S] = p.transpose(0, 1, 3, 2)
    return {"pts": a.reshape(N, 128, X), "ld": np.stack([gtable(e) for e in ld]), "cp": np.stack([gtable(e.reshape(8, -1)) for e in cp]),
            "xs": np.stack([gtable(e) for e in xs]), "ys": np.stack([gtable(e) for e in ys])}
def setup_inputs(rng):
    p, ld, cp, xs, ys = parts(rng)
    return pack(p, ld, cp, name(rng, p, xs), ys)
def setup_inputs_alike(rng):
    p, ld, cp, xs, ys = parts(rng)
    own = np.stack([np.concatenate([r * V + np.arange(V), M + np.arange(U)]) for r in range(N)])
    p[:, 0, :V] = around(rng, numbers_of(), rng.integers(0, S, (N, 8, V)))[:, 0]
    ld[:, 0] = own; cp[:, 0] = own[:, None]; xs[:, 0] = own[:, :V]
    ld[:, 1] = rng.integers(0, M, (N, 1)); cp[:, 1] = rng.integers(0, M, (N, 1, 1)); xs[:, 1] = rng.integers(0, M, (N, 1)); ys[:, 1] = rng.integers(0, M, (N, 1))
    p[:, 2, :V] = around(rng, np.array([M // 3]), np.array([S // 2]))[0]
    ld[:, 3] = NONE; cp[:, 3] = NONE
    ld[:, 4] = rng.integers(M, M + U, (N, X))
    ld[:, 5] = rng.integers(0, V, (N, X)) + V * np.arange(N)[:, None]
    ld[:, 6] = rng.integers(0, V, (N, X)) + V * ((np.arange(N) + 1) % N)[:, None]
    cp[:, 7] = ld[:, 7][:, None]
    keep = name(rng, p, xs); xs[:, 2:] = keep[:, 2:]
    return pack(p, ld, cp, xs, ys)
def setup_inputs_chain(rng):
    p, ld, cp, xs, ys = parts(rng); p[:] = NONE; ld[:] = NONE; cp[:] = NONE; xs[:] = NONE
    h = M // 4; kind = rng.permutation(8)
    for g in kind[:4]:
        o = rng.permutation(M); hub, shelf, leaf, rest = o[:h], o[h:2 * h], np.sort(o[2 * h:3 * h]), o[3 * h:]
        p[leaf // V, g, leaf % V, 0] = np.sort(rng.permutation(M)[:h])
        pick = np.sort(rng.integers(0, h - S + 1, (h, S)), axis=1) + np.arange(S)
        p[shelf // V, g, shelf % V] = leaf[pick]
        p[hub // V, g, hub % V, 0] = leaf[pick[:, 0]]; cp[hub // V, g, C - 1, hub % V] = shelf
        ld[:, g, V:] = hub[rng.integers(0, h, (N, U))]; ld[rest // V, g, rest % V] = hub[rng.integers(0, h, len(rest))]
    for g in kind[4:6]:
        e = 2 * h; o = rng.permutation(e); hub, shelf = o[:h], o[h:]
        leaf = e + np.sort(rng.permutation(e - 1)[:h]); held = np.sort(rng.permutation(e)[:h])
        pick = np.sort(rng.integers(0, h - 2 * S + 2, (h, 2 * S - 1)), axis=1) + np.arange(2 * S - 1)
        i = rng.integers(0, h, (N, X)); ld[:, g] = hub[i]
        p[:, g, :, :S - 1] = held[pick[i][:, :, :S - 1]]
        p[leaf // V, g, leaf % V] = NONE; p[leaf // V, g, leaf % V, 0] = held; p[leaf // V, g, leaf % V, 1] = M - 1
        p[hub // V, g, hub % V] = leaf[pick[:, :S]]; cp[hub // V, g, C - 1, hub % V] = shelf
        p[shelf // V, g, shelf % V] = np.concatenate([leaf[pick[:, S:]], np.full((h, 1), M - 1)], axis=1)
    for g in kind[6:]:
        b = int(rng.integers(0, N)); b1 = (b + 1) % N; b2 = (b + 2) % N; half = U // 2
        p[b, g, V:] = np.sort(rng.integers(0, M - S + 1, (U, S)), axis=1) + np.arange(S)
        cp[b, g, C - 1, :V] = M + rng.integers(0, U, V)
        cp[b1, g, C - 1] = b * V + rng.integers(0, V, X)
        cp[b2, g, C - 1] = b1 * V + rng.integers(0, V, X)
        for d in range(3, N):
            q = (b + d) % N
            p[q, g, V:V + half, 0] = rng.integers(0, M, half)
            cp[q, g, C - 1, :V] = M + rng.integers(0, half, V)
            cp[q, g, C - 1, V + half:] = b1 * V + rng.integers(0, V, U - half)
    return pack(p, ld, cp, xs, ys)
def setup_inputs_ends(rng):
    p, ld, cp, xs, ys = parts(rng)
    e = np.full((8, S), NONE); e[1, 0] = 0; e[2, 0] = M - 1; e[3, :2] = (0, M - 1); e[4] = np.arange(S); e[5] = M - S + np.arange(S); e[6, :2] = (V - 1, V); e[7, 0] = 1
    p = np.where((rng.random((N, 8, X)) < 0.7)[..., None], e[rng.integers(0, 8, (N, 8, X))], p)
    ends = np.array([0, V - 1, V, M - 1, M, NONE - 1, NONE]); xs = name(rng, p, xs)
    ld, cp, ys = [np.where(rng.random(a.shape) < 0.4, ends[rng.integers(0, 7, a.shape)], a) for a in (ld, cp, ys)]
    xs = np.where(rng.random(xs.shape) < 0.3, ends[rng.integers(0, 7, xs.shape)], xs)
    return pack(p, ld, cp, xs, ys)
def full_stores(rng, g, p, ld, cp, xs, ys):
    b = N - 1; low = M - V; to = rng.permutation(V)
    hr = (np.arange(b)[:, None] + rng.integers(1, b)) % b
    ld[:, g, :2 * V] = NONE; cp[:, g, :, :2 * V] = NONE
    p[hr, g, to] = hold(rng, np.arange(low).reshape(b, V), 0, low); xs[:b, g] = hr * V + to
    p[b, g, :V] = hold(rng, low + np.arange(V), low, M); ys[:b, g] = low + rng.integers(0, V, (b, V))
    xs[b, g] = rng.integers(0, low, V); ys[b, g] = rng.integers(0, low, V)
    nx = np.append((np.arange(b) + 1) % b, 0)
    p[:, g, V:2 * V] = p[nx, g, :V]; cp[:, g, C - 1, V:2 * V] = nx[:, None] * V + np.arange(V)
def late_names(rng, g, p, ld, cp, xs, ys):
    H = V // 3; Q = (V - 2 * H) // 2; ra = np.arange(N)[:, None]; k = np.arange(H)
    pm = np.concatenate([1 + np.argsort(rng.random((N, V - 1)), axis=1), np.zeros((N, 1), np.int64)], axis=1)
    namer, quiet, source = pm[:, :H], pm[:, 2 * H:2 * H + Q], pm[:, 2 * H + Q:]
    ld[:, g, :V + H] = NONE; cp[:, g, :, :V + H] = NONE; ld[:, g, X - 1] = NONE; cp[:, g, :, X - 1] = NONE; xs[:, g] = NONE
    far = (ra + np.where(k // (RO - 1) % 2 == 1, rng.integers(1, N, H), 0)) % N
    feed = around(rng, ra * V + namer, k % (RO - 1)); hv = pm[far, H + k]; low = feed[..., 0]
    p[far, g, V + k] = feed; cp[far, g, C - 1, hv] = M + k + np.zeros((N, 1), np.int64)
    p[far, g, hv] = NONE; p[far, g, hv, 0] = np.where((low > 0) & (rng.random(low.shape) < 0.5), low - 1, NONE)
    xs[ra, g, namer] = far * V + hv
    p[ra, g, source] = hold(rng, ra * V + source, 0, M)
    p[0, g, 0] = np.sort(rng.permutation((ra * V + quiet).reshape(-1))[:S])
    p[:, g, X - 1] = np.sort(ra * V + quiet[:, :S], axis=1)
    ask = np.concatenate([namer, quiet], axis=1); away = (ra + rng.integers(1, N, ask.shape)) % N
    sv = source[away, rng.integers(0, source.shape[1], ask.shape)]
    ys[ra, g, ask] = away * V + sv
    p[ra, g, ask] = cut(p[away, g, sv], rng.integers(0, S, ask.shape))
def setup_inputs_stores(rng):
    p, ld, cp, xs, ys = parts(rng); o = numbers_of(); sh = (N, 8, V)
    case = rng.integers(0, 4, sh); mid = np.where(case == 2, np.where(o + 1 < M, o + 1, 0), o)
    x = around(rng, mid, np.where(case == 1, S - 1, 0))
    p[:, :, V:2 * V] = np.where((case == 3)[..., None], NONE, x)
    ld[:, :, V:2 * V] = np.where(case == 3, NONE, ld[:, :, V:2 * V]); cp[:, :, :, V:2 * V] = NONE
    cp[:, :, 0, V:2 * V] = np.where(case == 3, (o + V) % M, NONE)
    j = rng.integers(0, RO, sh); k = around(rng, o, j)
    k = cut(k, np.where(rng.random(sh) < 0.5, np.minimum(j, o) + 1, S)); p[:, :, :V] = np.roll(k, 1, axis=0)
    quiet = rng.random(sh) < 0.5
    ld[:, :, :V] = np.where(quiet, NONE, ld[:, :, :V]); cp[..., :V] = np.where(quiet[:, :, None], NONE, cp[..., :V])
    xs = M + np.arange(V) + np.zeros(sh, np.int64)
    kind = [int(g) for g in rng.permutation(8)]
    for g in kind[:2]: full_stores(rng, g, p, ld, cp, xs, ys)
    for g in kind[2:4]: late_names(rng, g, p, ld, cp, xs, ys)
    return pack(p, ld, cp, xs, ys)
def setup_inputs_spread(rng):
    p, ld, cp, xs, ys = parts(rng)
    x = np.minimum(np.exp2(np.log2(M - S + 1) * rng.random((N, 8, X, S))).astype(np.int64) - 1, M - S)
    x = np.sort(x, axis=-1) + np.arange(S); x = np.where(rng.random((N, 8, X, 1)) < 0.35, (M - 1 - x)[..., ::-1], x)
    p = cut(x, np.minimum((rng.random((N, 8, X)) ** 2 * (S + 1)).astype(np.int64), S))
    ld, cp, xs, ys = [np.minimum((rng.random(a.shape) ** 3 * (NONE + 1)).astype(np.int64), NONE) for a in (ld, cp, xs, ys)]
    return pack(p, ld, cp, name(rng, p, xs), ys)
def check_inputs(d):
    bad = []
    a = np.asarray(d["pts"]).reshape(N, 8, 16, X); h = a[:, :, :S]
    if not np.all(((h >= 0) & (h < M)) | (h == NONE)): bad.append("range of pts")
    if not np.all((h[:, :, 1:] > h[:, :, :-1]) | (h[:, :, 1:] == NONE)): bad.append("pts rises")
    if not np.all(a[:, :, S:] == NONE): bad.append("later slots of pts")
    for k in ("ld", "cp", "xs", "ys"):
        if np.min(d[k]) < 0 or np.max(d[k]) > NONE: bad.append("range of " + k)
    return bad
def reference(pts, ld, cp, xs, ys):
    p = pts.astype(np.int64).reshape(N, 8, 16, X)
    lds, cps, xss, yss = [np.stack([gentries(a) for a in b]).astype(np.int64) for b in (ld, cp, xs, ys)]
    cps = cps.reshape(N, 8, C, X)
    def take(w, ix):
        return np.take_along_axis(w, ix[:, None, :], 2)
    for t in range(RO):
        objects = np.concatenate([p[q, :, :, :V] for q in range(N)], axis=2); gain = []
        for a in range(N):
            w = np.concatenate([objects, p[a, :, :, V:], np.full((8, 16, 1), NONE)], axis=2)
            top = np.max(np.where(p[a] == NONE, -1, p[a]), axis=1)[:, None, :]
            best = np.full((8, X), NONE)
            edge = take(w, lds[a])
            for i in range(S + t):
                s = take(w, edge[:, i]); best = np.minimum(best, np.min(np.where(s > top, s, NONE), axis=1))
            for c in range(C):
                s = take(w, cps[a, :, c]); best = np.minimum(best, np.min(np.where(s > top, s, NONE), axis=1))
            named = np.any(take(w, xss[a]) == a * V + np.arange(V), axis=1)[:, None, :]
            s = take(w, yss[a]); s = np.min(np.where(named & (s > top[:, :, :V]), s, NONE), axis=1)
            best[:, :V] = np.minimum(best[:, :V], s); gain.append(best)
        p[:, :, S + t] = np.stack(gain)
    return {"yp": p.reshape(N, 128, X).astype(np.float32)}

@@ -1,0 +1,557 @@
+from concourse.bass import DstId, RemoteDMATransfer
+from concourse.mybir import AluOpType as A, ActivationFunctionType as F
+
+NR, V, RO = 4, 512, 4
+OB = 520
+EW = 512
+WW = 2576
+NSRC = sum(10 + t + 9 + t for t in range(RO))
+ZS, ZW = 6, 768
+PATS = [(10, 2304.0), (12, 2304.0), (14, 2560.0), (12, 2560.0)]
+
+
+def _sb(n, dt):
+    return ("sbuf", [128, n], dt)
+
+
+SCRATCH = {
+    "pi": _sb(512, "int32"), "pk": _sb(256, "int32"), "k16": _sb(256, "float16"), "sh": _sb(128, "bfloat16"),
+    "bz": _sb(8, "float32"), "bz0": _sb(8, "float32"),
+    "li": _sb(192, "int32"), "lt": _sb(192, "float32"), "lu": _sb(192, "float32"),
+    "lo": _sb(192, "uint16"), "eo": _sb(11 * 64, "uint16"),
+    "p16": _sb(1024, "float16"), "sc": _sb(1024, "float16"), "land": _sb(1024, "float16"), "scl": _sb(2048, "float16"),
+    "hl": _sb(3 * 512, "float16"), "out0": _sb(1024, "float32"),
+    "w0": _sb(WW, "float32"), "w1": _sb(WW, "float32"), "w2": _sb(WW, "float32"), "w3": _sb(WW, "float32"),
+    "m": _sb(NSRC * 512, "float16"), "z": _sb(ZS * ZW, "float16"), "top": _sb(8 * 512, "float16"),
+    "xl": _sb(4 * 1024, "float16"), "xx": _sb(4 * 512, "float16"), "ab": _sb(256, "float32"), "zx": _sb(11 * 32, "float16"),
+    "pen": _sb(4 * 32, "float16"), "so": _sb(8 * 448, "float16"), "u": _sb(8 * 32, "float16"),
+    "h0": _sb(128, "float16"), "h1": _sb(128, "float16"), "go": _sb(8 * 128, "float32"),
+    "t1": _sb(256, "float16"), "t2": _sb(256, "float16"), "t3": _sb(128, "float16"), "a0": _sb(64, "float16"), "u0": _sb(64, "float16"),
+    "zero": _sb(512, "bfloat16"), "big": _sb(32, "float16"), "ident": _sb(128, "bfloat16"), "nid": _sb(128, "bfloat16"),
+    "keep": _sb(128, "bfloat16"), "pick": _sb(96, "bfloat16"), "yc": _sb(96, "bfloat16"), "y0c": _sb(64, "bfloat16"),
+    "selt": _sb(608, "bfloat16"), "selw": _sb(512, "bfloat16"), "am": _sb(11 * 144, "bfloat16"),
+    "ownf": _sb(256, "float32"), "own": _sb(256, "float16"), "ki": _sb(8, "int32"), "qi": _sb(8, "int32"),
+    "jf": _sb(8, "float32"), "bw0": _sb(8, "float32"), "bw": _sb(8, "float32"), "sw": _sb(8, "float32"), "qf": _sb(8, "float32"),
+    "b14": _sb(8, "float32"), "be": _sb(8, "float32"), "bo": _sb(8, "float32"), "kp": _sb(8, "float32"),
+    "rs0": _sb(448, "float16"), "rs1": _sb(448, "float16"), "rs2": _sb(448, "float16"), "rs3": _sb(448, "float16"),
+}
+for _b in ("y0", "y1", "y2", "q0", "q1", "m1", "m2", "m3"):
+    SCRATCH[_b] = ("psum", [128, 512], "float32")
+SEMAPHORES = ["dve", "act", "pe", "pool", "ldo", "ldt", "ldl", "rep", "o0", "outs", "ar0", "ar1", "ar2", "ar3", "ar4",
+              "sent0", "sent1", "sent2", "sent3", "sent4"]
+
+PAR = dict(cy=1.04, ga=1.56, pc=0.52, hop=100.0, look=60.0, ao=100.0, vo=40.0, rem=("act", "dve", "act"), lat0=4700.0, lat=3200.0,
+           ldt=0.94, toppr=0.02, tries=100, moves=16000)
+CASES = [dict(ga=1.1, ao=70.0, pc=.45, lat=2800.0), dict(ga=1.3, ao=100.0, pc=.52, lat=3500.0), dict(ga=1.56, ao=80.0, pc=.52, lat=3200.0),
+         dict(ga=1.56, ao=80.0, pc=.7, lat=3200.0), dict(ga=1.8, ao=120.0, pc=.6, lat=4500.0), dict(ga=2.05, ao=80.0, pc=.52, lat=3500.0)]
+KEPT = {}
+
+
+def dve(n, f=1.0):
+    return PAR["vo"] + max(64, n * f) * PAR["cy"]
+
+
+def act(n, f=1.0):
+    return PAR["ao"] + max(64, n * f) * PAR["cy"]
+
+
+def pool(n):
+    return 150 + 2 * n * PAR["cy"]
+
+
+def plan(g, core, T, topo, rank):
+    S = T.sem
+    GA = PAR["ga"]
+    Vq, Cq, Pq, Yq = g.vector, g.scalar, g.tensor, g.sync
+    ops, last_w, readers = [], {}, {}
+
+    def op(eng, fn, cost, r=(), w=(), prio=0.0, lat=0.0, sem=None):
+        i = len(ops)
+        deps, war = set(), set()
+        for k in r:
+            if k in last_w:
+                deps.add(last_w[k])
+        for k in w:
+            if k in last_w:
+                deps.add(last_w[k])
+            war.update(readers.get(k, ()))
+        for k in r:
+            readers.setdefault(k, []).append(i)
+        for k in w:
+            last_w[k] = i
+            readers[k] = []
+        war -= deps
+        deps |= war
+        deps.discard(i)
+        ops.append(dict(eng=eng, fn=fn, cost=cost, deps=deps, war=war, prio=prio, lat=lat, sem=sem))
+        return i
+
+    def mm(group, r, w, prio):
+        def fn():
+            ins = None
+            for (o, l, rh, st, sp, _m, _n) in group:
+                ins = Pq.matmul(o, l, rh, st, sp)
+            return ins
+        return op("pe", fn, sum(max(min(64, x[5]), x[6]) for x in group) * PAR["pc"], r, w, prio)
+
+    W = [T.w0, T.w1, T.w2, T.w3]
+    H = [T.h0, T.h1]
+    Y = ["y0", "y1", "y2"]
+    others = [q for q in range(NR) if q != rank]
+    peers = [T.cores[q] for q in others]
+    mask = -1
+    for c in peers:
+        mask &= topo.mask(core, c)
+    dsts = [DstId(rid=topo.addr(c)[0], pnc=topo.addr(c)[1]) for c in peers]
+    own0 = OB + V * rank
+
+    def wblock(t, ph):
+        return W[t][:, own0:own0 + V] if ph == 0 else W[t][:, 0:V]
+
+    def send(k, src, dst, r, prio, lat):
+        def fn():
+            g.remote_dma_fused([RemoteDMATransfer(dst_ids=dsts, dma_engine_mask=mask, remote_sem=S["ar%d" % k],
+                                                  srcs=[src], dsts=[dst] * len(dsts))], local_sem=S["sent%d" % k])
+            return None
+        ne = bin(mask).count("1")
+        op("pool", fn, 500, r, [("arr", k)], prio, lat, sem=("ar%d" % k, ne * len(dsts), False, "sent%d" % k, ne))
+
+    for i in range(8):
+        e, q = (("sync", Yq), ("act", Cq))[i % 2]
+        op(e, lambda i=i, q=q: q.dma_start(T.pk[i::8, :], T.pts[i::16, 0:V]), 60, [], [("pk", i)], -110 + i, 2500, ("ldo", 128, True))
+    op("sync", lambda: Yq.dma_start(T.pi[:], T.pts[:, V:]), 60, [], ["piT"], -99.5, 3600, ("ldt", 16, True))
+    for j, (nm, a, b) in enumerate([("ld", 0, 64), ("cp", 64, 128), ("xs", 128, 160), ("ys", 160, 192)]):
+        op("act", lambda nm=nm, a=a, b=b: Cq.dma_start(T.li[:, a:b], T[nm][:]), 60, [], [("li", j)], -99 + j, 2200, ("ldl", 64, True))
+
+    def sel(out, in_, pattern, fill, base, r, w, prio, n):
+        op("pool", lambda: g.affine_select(out, in_, pattern, A.not_equal, fill, base, -1), pool(n), r, w, prio)
+
+    def col(out, in0, s1, s2, o0, o1, r, w, prio):
+        if o1 is None:
+            op("dve", lambda: Vq.tensor_scalar(out, in0, s1, None, o0), dve(1), r, w, prio)
+        else:
+            op("dve", lambda: Vq.tensor_scalar(out, in0, s1, s2, o0, o1), dve(1), r, w, prio)
+
+    q1 = T.qi[:, 0:1]
+    op("dve", lambda: Vq.memset(T.zero[:], 0.0), dve(512, .5), [], ["zero"], -100)
+    op("pool", lambda: g.iota(T.ki[:, 0:1], [[0, 1]], 0, 1), 140, [], ["ki"], -100)
+    op("pool", lambda: g.iota(T.jf[:, 0:4], [[1, 4]], 8, 0, allow_small_or_imprecise_dtypes=True), 140, [], ["jf"], -99)
+    col(q1, T.ki[:, 0:1], 15, None, A.bitwise_and, None, ["ki"], ["qi"], -99)
+    col(T.b14[:, 0:1], q1, 14.0, 2563.0, A.is_ge, A.mult, ["qi"], ["b14"], -98)
+    col(T.be[:, 0:1], T.b14[:, 0:1], -1.0, 2562.0, A.mult, A.add, ["b14"], ["be"], -97)
+    op("dve", lambda: Vq.tensor_copy(T.qf[:, 0:1], q1), dve(1), ["qi"], ["qf"], -75)
+    col(T.bo[:, 0:1], q1, 14.0, 2561.0, A.is_ge, A.mult, ["qi"], ["bo"], -72)
+    col(T.kp[:, 0:1], q1, 7.0, None, A.is_lt, None, ["qi"], ["kp"], -60)
+    col(T.bw0[:, 0:4], T.jf[:, 0:4], T.qf[:, 0:1], 2562.0, A.is_le, A.mult, ["jf", "qf"], ["bw0"], -59)
+    col(T.bw[:, 0:4], T.bw0[:, 0:4], T.b14[:, 0:1], None, A.subtract, None, ["bw0", "b14"], ["bw"], -58)
+    col(T.sw[:, 0:4], T.jf[:, 0:4], T.qf[:, 0:1], None, A.is_gt, None, ["jf", "qf"], ["sw"], -68)
+    col(T.bz0[:, 0:1], q1, 8.0, 2560.0, A.is_ge, A.mult, ["qi"], ["bz0"], -70)
+    col(T.bz[:, 0:1], T.bz0[:, 0:1], T.bo[:, 0:1], None, A.subtract, None, ["bz0", "bo"], ["bz"], -69)
+    op("dve", lambda: Vq.memset(T.h0[:], 0.0), dve(128, .5), [], [("h", 0, x) for x in range(4)], -61)
+    op("dve", lambda: Vq.memset(T.big[:], 4096.0), dve(32), [], ["big"], -57)
+    for j, (e, val) in enumerate(PATS):
+        rs = T["rs%d" % j]
+        op("dve", lambda rs=rs, e=e: Vq.memset(rs[:, 0:32 * e], -4.0), dve(32 * e, .5), [], [("rs", j)], -56 + j)
+        op("dve", lambda rs=rs, e=e, val=val: Vq.memset(rs[:, 0:32 * e:e], val), dve(32), [], [("rs", j)], -56 + j)
+    sel(T.pick[:], T.zero[:, 0:96], [[1, 12], [16, 8]], 1.0, 0, ["zero"], ["pick"], -98, 96)
+    sel(T.y0c[:], T.pick[:, 0:64], [[1, 8], [16, 8]], -8.0, 1, ["pick"], ["y0c"], -97, 64)
+    sel(T.y0c[:], T.y0c[:], [[0, 8], [16, 8]], 8.0, 9, ["y0c"], ["y0c"], -96, 64)
+    sel(T.ident[:], T.zero[:, 0:128], [[1, 128]], 1.0, 0, ["zero"], ["ident"], -95, 128)
+    sel(T.sh[:], T.zero[:, 0:128], [[1, 128]], 1.0, 8, ["zero"], ["sh"], -94.5, 128)
+    sel(T.selt[0:32, 0:512], T.zero[0:32, 0:512], [[1, 4], [4, 8], [0, 16]], 1.0, 0, ["zero"], ["selt0"], -94, 512)
+    sel(T.selt[0:32, 512:576], T.zero[0:32, 0:64], [[1, 32], [0, 2]], 1.0, 0, ["zero"], ["i20"], -80, 64)
+    sel(T.selt[0:32, 576:608], T.zero[0:32, 0:32], [[1, 32]], -1.0, 0, ["zero"], ["ni0"], -80, 32)
+    for j in range(1, 4):
+        op("sync", lambda j=j: Yq.dma_start(T.selt[32 * j:32 * j + 32, :], T.selt[0:32, :]), 60, ["selt0", "i20", "ni0"], [("rep", j)],
+           -50, 2000, ("rep", 48, True))
+    sel(T.yc[:, 8:96], T.pick[:, 8:96], [[1, 11], [16, 8]], -4096.0, 0, ["pick"], ["yc"], -79, 88)
+    sel(T.yc[:, 8:96], T.yc[:, 8:96], [[0, 11], [16, 8]], 4096.0, 14, ["yc"], ["yc"], -78, 88)
+    sel(T.yc[:, 8:96], T.yc[:, 8:96], [[0, 11], [16, 8]], -1.0, 15, ["yc"], ["yc"], -77, 88)
+    sel(T.yc[:, 0:8], T.pick[:, 0:8], [[16, 8]], -1.0, 15, ["pick"], ["ycb"], -76, 8)
+    for s in range(11):
+        sel(T.am[:, 144 * s:144 * s + 144], T.zero[:, 0:144], [[16, 9], [1000, 16]], 1.0, s - 15000, ["zero"], [("am", s)],
+            -70 + s if s < 8 else -40 + s, 144)
+    op("pool", lambda: g.iota(T.ownf[:], [[0, 64], [-128, 4]], -V * rank, -1, allow_small_or_imprecise_dtypes=True), pool(256), [], ["ownf"], -55)
+    sel(T.nid[:], T.zero[:, 0:128], [[1, 128]], -1.0, 0, ["zero"], ["nid"], -54, 128)
+    op("pool", lambda: g.affine_select(T.selw[:], T.selt[:, 0:512], [[0, 32], [32, 16]], A.is_ge, 0.0, -193, -1),
+       pool(512), ["selt0"] + [("rep", j) for j in range(1, 4)], ["selw"], -53)
+    op("act", lambda: Cq.activation(T.own[:], T.ownf[:], F.Identity), act(256), ["ownf"], ["own"], -5)
+    col(T.keep[:], T.ident[:], T.kp[:, 0:1], None, A.mult, None, ["ident", "kp"], ["keep"], -50)
+    for t in range(RO):
+        for j, a in enumerate((EW, WW - 8)):
+            op("act", lambda t=t, a=a: Cq.activation(W[t][:, a:a + 8], T.zero[:, 0:8], F.Identity, bias=T.be[:, 0:1]), act(8),
+               ["zero", "be"], [("wE", t, j)], -90 + t)
+
+    def widen(src, r, parts, prio):
+        for h, bank, c0, eng, outs in parts:
+            mm([(T[bank][:, c0:c0 + 256], (T.ident, T.sh)[h][:], src, True, True, 128, 256)], r + ["ident", "sh", bank], [], prio)
+        for h, bank, c0, eng, outs in parts:
+            for out, n, key in outs:
+                if eng == "act":
+                    op("act", lambda out=out, bank=bank, n=n: Cq.activation(out, T[bank][:, 0:n], F.Identity, bias=T.bz[:, 0:1], scale=T.sw[:, 0:1]),
+                       act(n), ["bz", "sw"], [bank, key], prio)
+                else:
+                    op("dve", lambda out=out, bank=bank, n=n: Vq.tensor_scalar(out, T[bank][:, 0:n], T.sw[:, 0:1], T.bz[:, 0:1], A.mult, A.add),
+                       dve(n), ["bz", "sw"], [bank, key], prio)
+
+    op("dve", lambda: Vq.tensor_copy(T.k16[:], T.pk[:]), dve(256), [("pk", i) for i in range(8)], ["k16"], -200)
+    send(0, T.k16[:], T.land[:, 256 * rank:256 * rank + 256], ["k16"], -300, PAR["lat0"] - 1100)
+    op("dve", lambda: Vq.tensor_scalar(T.p16[:, V:], T.pi[:], T.be[:, 0:1], None, A.min), dve(512), ["piT", "be"], [("p16", 1)], -199)
+    widen(T.k16[:], ["k16"], [(0, "y1", 0, "act", []), (1, "y1", 256, "act", [(T.p16[:, 0:V], 512, ("p16", 0))])], -198)
+    for ph in range(2):
+        op("act", lambda ph=ph: Cq.activation(wblock(0, ph), T.p16[:, V * ph:V * ph + V], F.Identity), act(512), [("p16", ph)], [("w", 0, ph)], -30 + ph)
+    op("act", lambda: Cq.activation(T.out0[:], T.p16[:], F.Identity, bias=T.bo[:, 0:1]), act(1024), [("p16", 0), ("p16", 1), "bo"], ["out0"], -4)
+    op("sync", lambda: Yq.dma_start(T.yp[:], T.out0[:]), 60, ["out0"], ["yp0"], -4, 3000, ("o0", 16, True))
+    op("dve", lambda: Vq.tensor_scalar(T.lt[:], T.li[:], 2048.0, -2568.0, A.is_ge, A.mult), dve(192), [("li", j) for j in range(4)], ["lt"], -145.5)
+    op("dve", lambda: Vq.tensor_tensor(T.lu[:], T.lt[:], T.li[:], A.add), dve(192, 2), ["lt"], ["lu"], -44)
+    op("dve", lambda: Vq.tensor_scalar(T.lo[:], T.lu[:], float(OB), None, A.add), dve(192), ["lu"], ["lo"], -43)
+    mm([(T.y0[:, 2 * c + ph:512:8], T.p16[:, V * ph + 128 * c:V * ph + 128 * c + 128], T.y0c[:], True, True, 128, 64)
+        for ph in range(2) for c in range(4)], [("p16", 0), ("p16", 1), "y0c", "y0"], [], -150)
+    op("dve", lambda: Vq.tensor_copy(T.t1[:], T.y0[:, 256:512]), dve(256), [], ["y0", "t1"], -149)
+    op("dve", lambda: Vq.tensor_tensor(T.t2[:], T.y0[:, 0:256], T.t1[:], A.min), dve(256), ["t1"], ["y0", "t2"], -148)
+    op("dve", lambda: Vq.tensor_tensor(T.t3[:], T.t2[:, 0:128], T.t2[:, 128:256], A.min), dve(128, 2), ["t2"], ["t3"], -147)
+    op("dve", lambda: Vq.tensor_tensor(T.a0[:], T.t3[:, 0:64], T.t3[:, 64:128], A.min), dve(64, 2), ["t3"], ["a0"], -146)
+    op("dve", lambda: Vq.tensor_scalar(T.u0[:], T.a0[:], 2304.0, -4864.0, A.is_ge, A.mult), dve(64), ["a0"], ["u0"], -145)
+    mm([x for ph in range(2) for x in (
+        (T.m1[0:32, 128 * ph:128 * ph + 128], T.a0[:, ph::2], T.ident[:], True, False, 32, 128),
+        (T.m1[0:32, 128 * ph:128 * ph + 128], T.u0[:, ph::2], T.ident[:], False, True, 32, 128))],
+       ["a0", "u0", "ident", "m1"], [], -144)
+    for ph in range(2):
+        op("dve", lambda ph=ph: Vq.tensor_scalar(H[ph][0:32, :], T.m1[0:32, 128 * ph:128 * ph + 128], -1.0, None, A.max),
+           dve(128), [], ["m1", ("h", ph, 0)], -143 + ph)
+
+    def tcol(t, ph):
+        n = 2 * t + ph
+        return T.top[:, V * n:V * n + V]
+
+    def hkeys(ph, j):
+        return [("h", ph, x) for x in range(j + 1)] + ["selt0", "i20", "ni0"] + [("rep", x) for x in range(1, j + 1)]
+
+    def build_block(j, out, st, hist, r, w, bank, prio, eng):
+        mm([(T[bank][:], T.keep[:], st, True, False, 128, 512)] +
+           [(T[bank][:, 128 * c:128 * c + 128], T.selw[0:32 * j + 32, 128 * c:128 * c + 128], hist, False, c == 3, 128, 128)
+            for c in range(4)], r + ["keep", bank, "selw"], [], prio)
+        if eng == "act":
+            op("act", lambda: Cq.activation(out, T[bank][:], F.Identity, bias=T.bw[:, j:j + 1], scale=T.sw[:, j:j + 1]), act(512),
+               ["bw", "sw"], [bank, w], prio)
+        else:
+            op("dve", lambda: Vq.tensor_scalar(out, T[bank][:], T.sw[:, j:j + 1], T.bw[:, j:j + 1], A.mult, A.add), dve(512),
+               ["bw", "sw"], [bank, w], prio)
+
+    def build_top(j, ph, bank, prio):
+        mm([(T[bank][:, 128 * c:128 * c + 128], T.selt[0:32 * j + 32, 128 * c:128 * c + 128], H[ph][0:32 * j + 32, :], True, True, 128, 128)
+            for c in range(4)], hkeys(ph, j)[:j + 2] + [("rep", x) for x in range(1, j + 1)] + [bank], [], prio)
+        op("act", lambda: Cq.activation(tcol(j, ph), T[bank][:], F.Identity), act(512), [], [bank, ("top", j, ph)], prio)
+
+    for ph, bank in enumerate(("m2", "m3")):
+        build_top(0, ph, bank, -140 + ph)
+        op("dve", lambda ph=ph, bank=bank: Vq.tensor_tensor(T.sc[:, V * ph:V * ph + V], T[bank][:], T.p16[:, V * ph:V * ph + V], A.min),
+           dve(512), [("p16", ph)], [bank, ("sc", ph)], -42 + ph)
+    send(4, T.sc[:, 0:V], T.scl[:, V * rank:V * rank + V], [("sc", 0)], -60.5, PAR["lat0"])
+    qa, qb, qc = others
+
+    def wq(q, a, b):
+        return T.w0[:, OB + V * q + a:OB + V * q + b]
+
+    def lq(q):
+        return T.land[:, 256 * q:256 * q + 256]
+
+    widen(lq(qa), [("arr", 0)], [(0, "y1", 0, "act", []), (1, "y1", 256, "act", [(wq(qa, 0, V), 512, ("wr", 0))])], -252)
+    widen(lq(qb), [("arr", 0)], [(0, "y2", 0, "dve", []), (1, "y2", 256, "dve", [(wq(qb, 0, V), 512, ("wr", 1))])], -251)
+    widen(lq(qc), [("arr", 0)], [(0, "q0", 0, "act", [(wq(qc, 0, 256), 256, ("wr", 2))]), (1, "q1", 0, "dve", [(wq(qc, 256, V), 256, ("wr", 3))])], -250)
+
+    def wkeys(t, full):
+        k = [("w", t, 0), ("wE", t, 0), ("wE", t, 1)]
+        k += [("wr", j) for j in range(4)] if t == 0 else [("wq", t, x) for x in range(NR - 1)]
+        return k + ([("w", t, 1)] if full else [])
+
+    def lists(t, edges, c0, n, bank, prio):
+        grp = []
+        for i, s in enumerate(edges):
+            for r in range(16):
+                a = 1024 * t + 16 * c0 + r
+                grp.append((T[bank][:, n * i:n * i + n], T.am[:, 144 * s + 15 - r:144 * s + 143 - r], T.xl[:, a:1024 * t + 16 * (c0 + n):16],
+                            r == 0, r == 15, 128, n))
+        phs = [0, 1] if n == 64 else [c0 // 32]
+        mm(grp, [("xl", t, p) for p in phs] + [("am", s) for s in edges] + [bank], [], prio)
+        e0 = 64 * edges[0] + c0
+        op("dve", lambda: Vq.tensor_scalar(T.eo[:, e0:e0 + n * len(edges)], T[bank][:, 0:n * len(edges)], 8.0, 2056.0, A.add, A.min),
+           dve(n * len(edges)), [], [bank] + [("eo", s, p) for s in edges for p in phs], prio)
+
+    def load_sets(t, ph, prio):
+        op("act", lambda: Cq.activation(T.xl[:, 1024 * t + V * ph:1024 * t + V * ph + V], W[t][:].indirect(T.lo[:, 32 * ph:32 * ph + 32]), F.Identity),
+           act(512, GA), wkeys(t, True) + ["lo"], [("xl", t, ph)], prio)
+
+    cnt = dict(m=0, y=1, z=0)
+    for t in range(RO):
+        R = 9 + t
+        if t == 0:
+            for ph in range(2):
+                load_sets(0, ph, -3 + .1 * ph)
+            lists(0, [0], 0, 32, "m2", -2)
+            for edges, bank, pr in (([1], "m3", -1.9), ([2, 3], "m1", -1.89), ([4, 5], "m2", .01), ([6, 7], "m3", .11)):
+                lists(0, edges, 0, 64, bank, pr)
+            lists(0, [0], 32, 32, "m1", .3)
+        else:
+            for ph in range(2):
+                pr = 2 * t - 0.06 if ph == 0 else 2 * t + PAR["ldt"]
+                load_sets(t, ph, pr)
+                lists(t, [7 + t], 32 * ph, 32, "m2", pr)
+        s0, P = (0, 8) if t == 0 else (7 + t, 1)
+        pr = 2 * t - 0.05
+        op("act", lambda t=t: Cq.activation(T.xx[:, V * t:V * t + V], W[t][:].indirect(T.lo[:, 128:160]), F.Identity), act(512, GA),
+           wkeys(t, True) + ["lo"], [("xx", t)], pr)
+        mm([(T.m3[:, 0:32 * P], T.ident[:], T.own[:, 0:32 * P], True, False, 128, 32 * P)] +
+           [(T.m3[:, c:32 * P:4], T.xx[:, V * t + 128 * c:V * t + 128 * c + 128], T.pick[:, 8 * s0:8 * (s0 + P)], False, c == 3, 128, 8 * P)
+            for c in range(4)], [("xx", t), "own", "ident", "pick", "m3"], [], pr)
+        op("act", lambda P=P: Cq.activation(T.ab[:, 0:32 * P], T.m3[:, 0:32 * P], F.Abs), act(32 * P), [], ["m3", "ab"], pr)
+        op("act", lambda P=P, s0=s0: Cq.activation(T.zx[:, 32 * s0:32 * (s0 + P)], T.ab[:, 0:32 * P], F.Relu, bias=4096.0, scale=-4096.0),
+           act(32 * P), ["ab"], [("zx", t)], pr)
+        mm([(T.m3[:, 256:288], T.ident[:], T.zx[:, 32 * p:32 * p + 32], p == 0, p == 7 + t, 128, 32) for p in range(8 + t)],
+           [("zx", x) for x in range(t + 1)] + ["ident", "m3"], [], pr)
+        op("act", lambda t=t: Cq.activation(T.pen[:, 32 * t:32 * t + 32], T.m3[:, 256:288], F.Relu, bias=4096.0, scale=-1.0),
+           act(32), [], ["m3", ("pen", t)], pr)
+
+        for ph in range(2):
+            n = 2 * t + ph
+            old = list(range(8 if t == 0 else 7 + t))
+            places = ["cp", "ys"] if ph == 0 else ["cp"]
+            if t == 0:
+                order = ["cp"] + old[:5] + places[1:] + old[5:]
+                first = {"cp": -0.5, "ys": -0.45} if ph == 0 else {}
+            else:
+                order = old + places + [7 + t]
+                first = {}
+            E = len(order)
+            Ep = E + E % 2
+            pat = PATS.index((Ep, 2560.0 if t == RO - 1 else 2304.0))
+            Q = "q%d" % ph
+            half = Ep // 2
+            for gi in range(half):
+                srcs = order[2 * gi:2 * gi + 2]
+                zs = cnt["z"] % ZS
+                cnt["z"] += 1
+                zb = ZW * zs
+                for si, s in enumerate(srcs):
+                    pr = n + (2 * gi + si) / 20.0
+                    mi = cnt["m"]
+                    cnt["m"] += 1
+                    mt = T.m[:, 512 * mi:512 * mi + 512]
+                    if s == "cp":
+                        win, off, rk = W[t][:], T.lo[:, 64 + 32 * ph:96 + 32 * ph], wkeys(t, True) + ["lo"]
+                    elif s == "ys":
+                        win, off, rk = W[t][:], T.lo[:, 160:192], wkeys(t, True) + ["lo"]
+                    else:
+                        win, off, rk = W[t][:, EW:WW], T.eo[:, 64 * s + 32 * ph:64 * s + 32 * ph + 32], wkeys(t, False) + [("eo", s, ph)]
+                    op("dve", lambda mt=mt, win=win, off=off, t=t, ph=ph: Vq.tensor_tensor(mt, win.indirect(off), tcol(t, ph), A.max),
+                       dve(512, GA), rk + [("top", t, ph)], [("m", mi)], first.get(s, pr))
+                    yb = Y[cnt["y"] % 3]
+                    cnt["y"] += 1
+                    mm([(T[yb][:, c:32 * R:4], T.m[:, 512 * mi + 128 * c:512 * mi + 128 * c + 128], T.yc[:, 0:8 * R], True, True, 128, 8 * R)
+                        for c in range(4)], [("m", mi), "yc", "ycb", yb], [], pr)
+                    op("act", lambda yb=yb, zb=zb, si=si, R=R: Cq.activation(T.z[:, zb + si:zb + 64 * R:2], T[yb][:, 0:32 * R], F.Relu),
+                       act(32 * R), [], [yb, ("z", zs, si)], pr)
+                G = len(srcs)
+                st = 2 // G
+                qo = T[Q][:, gi:32 * Ep:half * st]
+                grp = [(qo, H[ph][0:32 * t + 32, :], T.selt[0:32 * t + 32, 512:576:st], True, False, 128, 32 * G)]
+                rk = hkeys(ph, t) + ["ident", Q] + [("z", zs, si) for si in range(G)]
+                if "ys" in srcs:
+                    a = gi + half * srcs.index("ys")
+                    grp.append((T[Q][:, a:32 * Ep:Ep], T.ident[:], T.pen[:, 32 * t:32 * t + 32], False, False, 128, 32))
+                    rk.append(("pen", t))
+                grp += [(qo, T.ident[:], T.z[:, zb + 64 * p:zb + 64 * p + 64:st], False, p == R - 1, 128, 32 * G) for p in range(R)]
+                if G == 1:
+                    grp.append((T[Q][:, gi + half:32 * Ep:Ep], T.ident[:], T.big[:], True, True, 128, 32))
+                    rk.append("big")
+                mm(grp, rk, [], n + (2 * gi + 1.5) / 20.0)
+            pr = n + 0.9
+            so = T.so[:, 448 * n:448 * n + 32 * Ep]
+            aa = T.so[:, 448 * n + Ep - 1:448 * n + 32 * Ep:Ep]
+            op("dve", lambda so=so, pat=pat, Ep=Ep, Q=Q: Vq.tensor_tensor_scan(so, T["rs%d" % pat][:, 0:32 * Ep], T[Q][:, 0:32 * Ep], 0.0, A.max, A.min),
+               dve(32 * Ep), [("rs", pat)], [Q, ("so", n)], pr)
+            j = (t + 1) % 4
+            p2 = T.m1[32 * j:32 * j + 32, 0:128]
+            gt = T.go[32 * j:32 * j + 32, 128 * n:128 * n + 128]
+            if t < RO - 1:
+                un = T.u[:, 32 * n:32 * n + 32]
+                pd = T.m1[32 * j:32 * j + 32, 128:256]
+                op("act", lambda un=un, aa=aa: Cq.activation(un, aa, F.Relu, bias=-38912.0, scale=19.0), act(32), [("so", n)], [("u", n)], pr)
+                mm([(pd, aa, T.ident[:], True, False, 32, 128), (pd, T.selt[0:32 * j, 576:608], H[ph][0:32 * j, :], False, False, 32, 128),
+                    (pd, un, T.nid[:], False, True, 32, 128),
+                    (p2, aa, T.ident[:], True, False, 32, 128), (p2, un, T.nid[:], False, True, 32, 128)],
+                   [("so", n), ("u", n), "ident", "nid", "m1"] + hkeys(ph, j - 1), [], pr)
+                op("act", lambda pd=pd, ph=ph, j=j: Cq.activation(H[ph][32 * j:32 * j + 32, :], pd, F.Relu), act(128), [], ["m1", ("h", ph, j)], pr)
+            else:
+                mm([(p2, aa, T.ident[:], True, True, 32, 128)], [("so", n), "ident", "m1"], [], pr)
+            op("act", lambda gt=gt, p2=p2: Cq.activation(gt, p2, F.Abs), act(128), [], ["m1", ("go", n)], pr + 0.022)
+            op("sync", lambda gt=gt, t=t, ph=ph: Yq.dma_start(T.yp[8 + t::16, V * ph:V * ph + V], gt), 60, [("go", n), "yp0"], [("yp", n)], pr + 0.03,
+               2000, ("outs", 16 * 2 * RO, True))
+            if t < RO - 1:
+                if ph == 0:
+                    a = 512 * (j - 1) + 128 * rank
+                    send(j, T.h0[:], T.hl[:, a:a + 128], [("h", 0, x) for x in range(4)], pr, PAR["lat"])
+                build_block(j, wblock(j, ph), T.sc[:, V * ph:V * ph + V], H[ph][0:32 * j + 32, :],
+                            [("h", ph, x) for x in range(j + 1)] + [("sc", ph)], ("w", j, ph), "m3", pr + 0.01, "act")
+                build_top(j, ph, "m2", pr + PAR["toppr"])
+                if ph == 0:
+                    for x, q in enumerate(others):
+                        a = 512 * (j - 1) + 128 * q
+                        build_block(j, W[j][:, OB + V * q:OB + V * q + V], T.scl[:, V * q:V * q + V], T.hl[0:32 * j + 32, a:a + 128],
+                                    [("arr", j), ("arr", 4)], ("wq", j, x), ("m3", "m2", "m1")[x], pr + 0.025, PAR["rem"][x])
+    return ops
+
+
+def schedule(ops):
+    n = len(ops)
+    users = [[] for _ in range(n)]
+    left = [len(o["deps"]) for o in ops]
+    for i, o in enumerate(ops):
+        for d in o["deps"]:
+            users[d].append(i)
+    ready = [0.0] * n
+    avail = {}
+    for i in range(n):
+        if left[i] == 0:
+            avail.setdefault(ops[i]["eng"], []).append(i)
+    free = {}
+    order = []
+    while len(order) < n:
+        best = None
+        for e, lst in avail.items():
+            if not lst:
+                continue
+            t0 = max(free.get(e, 0.0), min(ready[i] for i in lst))
+            i = min((i for i in lst if ready[i] <= t0 + PAR["look"]), key=lambda i: (ops[i]["prio"], i))
+            t0 = max(t0, ready[i])
+            if best is None or t0 < best[0]:
+                best = (t0, i, e)
+        t0, i, e = best
+        avail[e].remove(i)
+        free[e] = t0 + ops[i]["cost"]
+        order.append(i)
+        for u in users[i]:
+            ready[u] = max(ready[u], free[e] + ops[i]["lat"] + PAR["hop"])
+            left[u] -= 1
+            if left[u] == 0:
+                avail.setdefault(ops[u]["eng"], []).append(u)
+    return order
+
+
+def span(case, order):
+    hop = PAR["hop"]
+    free = dict(dve=0.0, act=0.0, pe=0.0, pool=0.0, sync=0.0)
+    done = [0.0] * len(order)
+    for i in order:
+        e, deps, cost, lat = case[i]
+        t0 = free[e]
+        for d in deps:
+            if done[d] > t0:
+                t0 = done[d]
+        free[e] = t0 + cost
+        done[i] = t0 + cost + lat + hop
+    return max(done)
+
+
+def choose(g, core, T, topo, rank):
+    if "order" in KEPT:
+        return plan(g, core, T, topo, rank), KEPT["order"]
+    base = dict(PAR)
+    cases = []
+    for c in CASES:
+        PAR.update(c)
+        cases.append([(o["eng"], tuple(o["deps"]), o["cost"], o["lat"]) for o in plan(g, core, T, topo, rank)])
+    seed = [12345]
+
+    def rnd():
+        seed[0] = (seed[0] * 1103515245 + 12345) % 2147483648
+        return seed[0] / 2147483648.0
+
+    def value(order):
+        val = 1.0
+        for c in cases:
+            val *= span(c, order) / 1e5
+        return val
+
+    best = None
+    for k in range(base["tries"]):
+        PAR.update(ga=1.25 + .65 * rnd(), ao=60 + 80 * rnd(), pc=.42 + .3 * rnd(), lat=2800 + 1500 * rnd(), look=40 + 200 * rnd())
+        ops = plan(g, core, T, topo, rank)
+        order = schedule(ops)
+        val = value(order)
+        if best is None or val < best[0]:
+            best = (val, ops, order)
+    PAR.update(base)
+    val, ops, order = best
+    n = len(order)
+    for k in range(base["moves"]):
+        a = int(rnd() * n)
+        e = ops[order[a]]["eng"]
+        b = a + 1
+        skip = int(rnd() * 2.5)
+        while b < n and (ops[order[b]]["eng"] != e or skip):
+            skip -= ops[order[b]]["eng"] == e
+            b += 1
+        if b >= n:
+            continue
+        seg = order[a:b + 1]
+        if rnd() < 0.5:
+            take = {seg[-1]}
+            for i in reversed(seg[:-1]):
+                if any(i in ops[u]["deps"] for u in take):
+                    take.add(i)
+            if seg[0] in take:
+                continue
+            new = [i for i in seg if i in take] + [i for i in seg if i not in take]
+        else:
+            take = {seg[0]}
+            for i in seg[1:]:
+                if ops[i]["deps"] & take:
+                    take.add(i)
+            if seg[-1] in take:
+                continue
+            new = [i for i in seg if i not in take] + [i for i in seg if i in take]
+        cand = order[:a] + new + order[b + 1:]
+        v = value(cand)
+        if v <= val:
+            val, order = v, cand
+    KEPT["order"] = order
+    return ops, order
+
+
+def rank_program(g, core, T, topo):
+    rank = T.rank_of(core)
+    if rank is None:
+        return
+    S = T.sem
+    ops, order = choose(g, core, T, topo, rank)
+    queue = dict(dve=g.vector, act=g.scalar, pe=g.tensor, pool=g, sync=g.sync)
+    needed = set(d for o in ops for d in o["deps"] if not (o["eng"] == "pe" and ops[d]["eng"] == "pe"))
+    count, token, seen = {}, {}, {}
+    for i in order:
+        o = ops[i]
+        e = o["eng"]
+        want = {}
+        for d in o["deps"]:
+            if e == "pe" and ops[d]["eng"] == "pe":
+                continue
+            sem = ops[d]["sem"]
+            s, v = sem[3:] if d in o["war"] and sem is not None and not sem[2] else token[d]
+            want[s] = max(want.get(s, 0), v)
+        for s in sorted(want):
+            if seen.get((e, s), 0) < want[s]:
+                queue[e].wait_ge(S[s], want[s])
+                seen[(e, s)] = want[s]
+        ins = o["fn"]()
+        if o["sem"] is not None:
+            if o["sem"][2]:
+                ins.then_inc(S[o["sem"][0]], 16)
+            token[i] = o["sem"][:2]
+        elif i in needed:
+            count[e] = count.get(e, 0) + 1
+            ins.then_inc(S[e], 1)
+            token[i] = (e, count[e])
+    g.sync.wait_ge(S.outs, 16 * 2 * RO)
+    for o in ops:
+        if o["sem"] is not None and not o["sem"][2]:
+            g.wait_ge(S[o["sem"][3]], o["sem"][4])

@@ -1,49 +1,58 @@
+import math
 from concourse.bass import DstId, RemoteDMATransfer
 from concourse.mybir import AluOpType as A, ActivationFunctionType as F
 
 NR, V, RO = 4, 512, 4
-OB = 520
-EW = 512
-WW = 2576
-NSRC = sum(10 + t + 9 + t for t in range(RO))
-ZS, ZW = 6, 768
-PATS = [(10, 2304.0), (12, 2304.0), (14, 2560.0), (12, 2560.0)]
+OB, EW, WW = 520, 512, 2568
+K, KD, MAGIC = 4096, 4096.0, 1.5 * 2.0 ** 35
+NPS, NX, L = (5, 6), 6, 11
+XW = 8 * NX * L
+NM = 12
+SN, SW = 512, 544
+XL = [9, 9, 10, 11]
+XO = [0, 0, 32 * NX * 9, 32 * NX * 19, 32 * NX * 30]
+GW = 32 * NX
+GAINED = [[], [9, 10, 13], [9, 10, 11, 14], [9, 10, 11, 12, 13]]
 
 
 def _sb(n, dt):
     return ("sbuf", [128, n], dt)
 
 
+H16, B16, F32 = "float16", "bfloat16", "float32"
 SCRATCH = {
-    "pi": _sb(512, "int32"), "pk": _sb(256, "int32"), "k16": _sb(256, "float16"), "sh": _sb(128, "bfloat16"),
-    "bz": _sb(8, "float32"), "bz0": _sb(8, "float32"),
-    "li": _sb(192, "int32"), "lt": _sb(192, "float32"), "lu": _sb(192, "float32"),
-    "lo": _sb(192, "uint16"), "eo": _sb(11 * 64, "uint16"),
-    "p16": _sb(1024, "float16"), "sc": _sb(1024, "float16"), "land": _sb(1024, "float16"), "scl": _sb(2048, "float16"),
-    "hl": _sb(3 * 512, "float16"), "out0": _sb(1024, "float32"),
-    "w0": _sb(WW, "float32"), "w1": _sb(WW, "float32"), "w2": _sb(WW, "float32"), "w3": _sb(WW, "float32"),
-    "m": _sb(NSRC * 512, "float16"), "z": _sb(ZS * ZW, "float16"), "top": _sb(8 * 512, "float16"),
-    "xl": _sb(4 * 1024, "float16"), "xx": _sb(4 * 512, "float16"), "ab": _sb(256, "float32"), "zx": _sb(11 * 32, "float16"),
-    "pen": _sb(4 * 32, "float16"), "so": _sb(8 * 448, "float16"), "u": _sb(8 * 32, "float16"),
-    "h0": _sb(128, "float16"), "h1": _sb(128, "float16"), "go": _sb(8 * 128, "float32"),
-    "t1": _sb(256, "float16"), "t2": _sb(256, "float16"), "t3": _sb(128, "float16"), "a0": _sb(64, "float16"), "u0": _sb(64, "float16"),
-    "zero": _sb(512, "bfloat16"), "big": _sb(32, "float16"), "ident": _sb(128, "bfloat16"), "nid": _sb(128, "bfloat16"),
-    "keep": _sb(128, "bfloat16"), "pick": _sb(96, "bfloat16"), "yc": _sb(96, "bfloat16"), "y0c": _sb(64, "bfloat16"),
-    "selt": _sb(608, "bfloat16"), "selw": _sb(512, "bfloat16"), "am": _sb(11 * 144, "bfloat16"),
-    "ownf": _sb(256, "float32"), "own": _sb(256, "float16"), "ki": _sb(8, "int32"), "qi": _sb(8, "int32"),
-    "jf": _sb(8, "float32"), "bw0": _sb(8, "float32"), "bw": _sb(8, "float32"), "sw": _sb(8, "float32"), "qf": _sb(8, "float32"),
-    "b14": _sb(8, "float32"), "be": _sb(8, "float32"), "bo": _sb(8, "float32"), "kp": _sb(8, "float32"),
-    "rs0": _sb(448, "float16"), "rs1": _sb(448, "float16"), "rs2": _sb(448, "float16"), "rs3": _sb(448, "float16"),
+    "pi": _sb(1024, "int32"), "x16": _sb(1024, H16), "u16": _sb(1024, H16), "pq": _sb(1024, H16), "land": _sb(2048, H16),
+    "li": _sb(192, "int32"), "lt": _sb(192, F32), "lu": _sb(192, F32), "lo": _sb(192, "uint16"), "eo": ("sbuf", [128, 2, 352], "uint16"),
+    "hl": _sb(3 * 512, H16), "out0": _sb(1024, F32), "w0": _sb(WW, F32), "w1": _sb(WW, F32), "w2": _sb(WW, F32), "w3": _sb(WW, F32),
+    "m": _sb(NM * 512, F32), "top": _sb(2 * 512, F32), "xl": _sb(4 * 1024, H16), "xx": _sb(4 * 512, H16), "ab": _sb(256, F32),
+    "zx": _sb(352, H16), "pen": ("sbuf", [128, 16, 16], H16), "so": _sb(8 * 256, H16), "sr": _sb(8 * GW, H16), "aa": _sb(256, H16), "u": _sb(256, H16),
+    "hb": _sb(512, F32), "rr": _sb(512, H16), "h0": _sb(128, H16), "h1": _sb(128, H16), "go": _sb(256, F32), "t0": _sb(512, H16),
+    "raw0": _sb(NX * 512, H16), "raw1": _sb(NX * 512, H16), "xt0": _sb(XO[RO], H16), "xt1": _sb(XO[RO], H16),
+    "xm0": ("sbuf", [128, GW, L], H16), "xm1": ("sbuf", [128, GW, L], H16), "seld": ("sbuf", [128, 32, NX * L], B16),
+    "ro0": _sb(4 * XW, H16), "ro1": _sb(4 * XW, H16), "pick9": _sb(72, B16), "db": _sb(1024, B16), "r0": _sb(256, B16), "e16": _sb(8, H16),
+    "gt": _sb(8 * GW, H16), "zb": _sb(2 * GW, F32), "zs": _sb(8 * GW, H16), "a1": _sb(256, H16),
+    "zero": _sb(XW, B16), "ident": _sb(128, B16), "nid": _sb(128, B16), "nkd": _sb(128, B16),
+    "dx": _sb(128, B16), "du": _sb(128, B16), "ws0": _sb(128, B16), "ws1": _sb(128, B16), "pick": _sb(64, B16),
+    "sel": _sb(SW, B16), "selw": _sb(512, B16), "am": _sb(8 * 144, B16), "ownf": _sb(8, F32), "own": _sb(256, B16),
+    "tab": _sb(256, F32), "mi": _sb(256, "int32"), "mj": _sb(256, "int32"), "mk": _sb(256, F32), "tm": _sb(256, F32), "tz": _sb(256, F32),
+    "ts": _sb(256, F32), "one": _sb(8, F32), "dg0": _sb(8, F32), "dg": _sb(8, F32), "sp": _sb(64, F32),
 }
-for _b in ("y0", "y1", "y2", "q0", "q1", "m1", "m2", "m3"):
-    SCRATCH[_b] = ("psum", [128, 512], "float32")
-SEMAPHORES = ["dve", "act", "pe", "pool", "ldo", "ldt", "ldl", "rep", "o0", "outs", "ar0", "ar1", "ar2", "ar3", "ar4",
-              "sent0", "sent1", "sent2", "sent3", "sent4"]
+for _e in range(3, 9):
+    SCRATCH["rs%d" % _e] = _sb(256, B16)
+GB, DB = ["g0", "g1", "g2"], ["d0", "d1", "d2"]
+for _b in DB:
+    SCRATCH[_b] = ("psum", [128, 512], F32)
+for _b in GB + ["q0", "q1"]:
+    SCRATCH[_b] = ("psum", [128, 8, 64], F32)
+SEMAPHORES = ["dve", "act", "pe", "pool", "ldo", "ldp", "ldt", "ldl", "rep", "o0", "outs", "ar0", "ar1", "ar2", "ar3",
+              "sent0", "sent1", "sent2", "sent3", "tp2", "tp3", "tp4", "tp5", "tp6", "tp7"]
 
-PAR = dict(cy=1.04, ga=1.56, pc=0.52, hop=100.0, look=60.0, ao=100.0, vo=40.0, rem=("act", "dve", "act"), lat0=4700.0, lat=3200.0,
-           ldt=0.94, toppr=0.02, tries=100, moves=16000)
-CASES = [dict(ga=1.1, ao=70.0, pc=.45, lat=2800.0), dict(ga=1.3, ao=100.0, pc=.52, lat=3500.0), dict(ga=1.56, ao=80.0, pc=.52, lat=3200.0),
-         dict(ga=1.56, ao=80.0, pc=.7, lat=3200.0), dict(ga=1.8, ao=120.0, pc=.6, lat=4500.0), dict(ga=2.05, ao=80.0, pc=.52, lat=3500.0)]
+PAR = dict(cy=.85, ga=1.56, pc=.43, po=0.0, hop=100.0, ao=70.0, vo=55.0, lat0=4200.0, lat=3000.0, dq=100.0, dlat=2300.0,
+           tries=40, starts=4, first=10000, steps=((20000, 200.0, 1.0), (20000, 80.0, 1.0)),
+           more=((80000, 100.0, 1.0), (80000, 50.0, .4), (60000, 30.0, .15)), marks=dict(arr=1.0, aa=0.3, wq=0.2),
+           cold=10.0, amp=4000.0, noise=3000.0, rem=(("act",) * 3,) * 3, x0=("act", "dve", "act", "dve"),
+           ob=(0, 0, 0, 0, 0, 0, 4, 3), wown="daaaaa", lde="aadadaaa", xse="aaaa", rd=[[4]] + [[]] * 7,
+           rg=([[0], [1], [2], [3], [4]], [[0, 1], [2, 3], [4, 5]]))
 KEPT = {}
 
 
@@ -56,7 +65,51 @@ def act(n, f=1.0):
 
 
 def pool(n):
-    return 150 + 2 * n * PAR["cy"]
+    return 170 + 2 * n * PAR["cy"]
+
+
+def table():
+    t = [[0.0] * 16 for _ in range(16)]
+    for r in range(RO):
+        for p in list(range(8)) + GAINED[r]:
+            t[r][p] = t[4 + r][p] = 1.0 - 2 * (p % 2)
+        t[r][8], t[4 + r][8] = (0.625 if r else 0.5), 0.3125
+    t[8], t[9] = [float(K)] * 16, [-1025.0 * K] * 16
+    t[8][8], t[9][8] = 0.0, 4096.0
+    t[10] = [0.0] * 8 + [1.0] * 8
+    t[11][8] = 1.0
+    for c in (12, 13):
+        t[c][:8] = [-1024.0 * K, -1025.0 * K] * 3 + [-1024.0 * K, 2048 - 1025.0 * K]
+    t[13][8:] = [-1.0, -1025.0 * K - 2049, -1025.0 * K, -1026.0 * K, -1025.0 * K, -1026.0 * K + 2561, -1025.0 * K - 2561, -1025.0 * K]
+    t[14] = [1.0] * 16
+    t[14][9] = t[14][14] = K + 1.0
+    t[14][13], t[14][15] = K - 1.0, float(K)
+    t[15] = [2048.0] * 8 + [2048.0 - K] * 8
+    return [x for c in t for x in c]
+
+
+def paints():
+    want = table()
+    base = [(0, 128, 2, 1.0), (1, 128, 2, -1.0), (128, 256, 1, 0.0)]
+    have = [1.0, -1.0] * 64 + [0.0] * 128
+    rest, used = [], set()
+    for val in sorted(set(want)):
+        need = set(i for i in range(256) if want[i] == val and have[i] != val)
+        while need:
+            best = None
+            for a in sorted(need):
+                for st in range(1, 130):
+                    n, hit = 0, 0
+                    while a + n * st < 256 and want[a + n * st] == val and a + n * st not in used:
+                        hit += a + n * st in need
+                        n += 1
+                    if best is None or hit > best[0]:
+                        best = (hit, a, st, n)
+            _, a, st, n = best
+            rest.append((a, a + (n - 1) * st + 1, st, val))
+            need -= set(range(a, a + n * st, st))
+            used |= set(range(a, a + n * st, st))
+    return base, rest
 
 
 def plan(g, core, T, topo, rank):
@@ -65,7 +118,7 @@ def plan(g, core, T, topo, rank):
     Vq, Cq, Pq, Yq = g.vector, g.scalar, g.tensor, g.sync
     ops, last_w, readers = [], {}, {}
 
-    def op(eng, fn, cost, r=(), w=(), prio=0.0, lat=0.0, sem=None):
+    def op(eng, fn, cost, r=(), w=(), prio=0.0, lat=0.0, sem=None, soft=()):
         i = len(ops)
         deps, war = set(), set()
         for k in r:
@@ -83,20 +136,67 @@ def plan(g, core, T, topo, rank):
         war -= deps
         deps |= war
         deps.discard(i)
-        ops.append(dict(eng=eng, fn=fn, cost=cost, deps=deps, war=war, prio=prio, lat=lat, sem=sem))
+        ops.append(dict(eng=eng, fn=fn, cost=cost, deps=deps, war=war, prio=prio, lat=lat, sem=sem, r=list(r), w=list(w),
+                        soft=set(last_w[k] for k in soft if k in last_w)))
         return i
 
-    def mm(group, r, w, prio):
+    def mm(group, r, w, prio, f=1):
         def fn():
             ins = None
             for (o, l, rh, st, sp, _m, _n) in group:
                 ins = Pq.matmul(o, l, rh, st, sp)
             return ins
-        return op("pe", fn, sum(max(min(64, x[5]), x[6]) for x in group) * PAR["pc"], r, w, prio)
+        return op("pe", fn, sum(PAR["po"] + f * max(min(64, x[5]), x[6]) * PAR["pc"] for x in group), r, w, prio)
+
+    def ac(out, in_, func, n, r, w, prio, f=1.0, **kw):
+        op("act", lambda: Cq.activation(out, in_, func, **kw), act(n, f), r, w, prio)
+
+    def ts(out, in_, a, b, o0, o1, n, r, w, prio, f=1.0):
+        if o1 is None:
+            op("dve", lambda: Vq.tensor_scalar(out, in_, a, None, o0), dve(n, f), r, w, prio)
+        else:
+            op("dve", lambda: Vq.tensor_scalar(out, in_, a, b, o0, o1), dve(n, f), r, w, prio)
+
+    def ev(eng, out, in_, n, r, w, prio, scale=1.0, bias=0.0):
+        if eng == "act":
+            ac(out, in_, F.Identity, n, r, w, prio, scale=scale, bias=bias)
+        else:
+            ts(out, in_, scale, bias, A.mult, A.add, n, r, w, prio)
+
+    def fill(out, val, n, w, prio, r=()):
+        op("dve", lambda: Vq.memset(out, val), dve(n), r, w, prio)
+
+    def tt(out, a, b, alu, n, r, w, prio, f=1.0):
+        op("dve", lambda: Vq.tensor_tensor(out, a, b, alu), dve(n, f), r, w, prio)
+
+    def scan(out, a, b, o0, o1, n, r, w, prio):
+        op("dve", lambda: Vq.tensor_tensor_scan(out, a, b, 0.0, o0, o1), dve(n), r, w, prio)
+
+    def sel(out, in_, pattern, val, base, r, w, prio, n, cm=-1):
+        op("pool", lambda: g.affine_select(out, in_, pattern, A.not_equal, val, base, cm), pool(n), list(r) + ["ps"], w, prio)
+
+    def iota(out, pattern, base, cm, w, prio, n):
+        op("pool", lambda: g.iota(out, pattern, base, cm, allow_small_or_imprecise_dtypes=True), pool(n), ["ps"], w, prio)
+
+    cnt = dict(m=0, g=0)
+    kinds = KEPT.setdefault("kind", {})
+
+    def bank(kind="g"):
+        cnt["g"] += 1
+        kinds[cnt["g"]] = kind
+        return cnt["g"]
+
+    def B(b):
+        return T[KEPT.get("bank", {}).get(b, "d0" if kinds[b] == "d" else "g0")]
+
+    def cols(b, a, n, p0=0, p1=128):
+        t = B(b)
+        if len(t.shape) == 2:
+            return t[p0:p1, a:a + n]
+        return t[p0:p1, a // 64:(a + n) // 64, :] if n >= 64 else t[p0:p1, a // 64, a % 64:a % 64 + n]
 
     W = [T.w0, T.w1, T.w2, T.w3]
-    H = [T.h0, T.h1]
-    Y = ["y0", "y1", "y2"]
+    H, RAW, XT, RS, XM = [T.h0, T.h1], [T.raw0, T.raw1], [T.xt0, T.xt1], [T.ro0, T.ro1], [T.xm0, T.xm1]
     others = [q for q in range(NR) if q != rank]
     peers = [T.cores[q] for q in others]
     mask = -1
@@ -104,6 +204,9 @@ def plan(g, core, T, topo, rank):
         mask &= topo.mask(core, c)
     dsts = [DstId(rid=topo.addr(c)[0], pnc=topo.addr(c)[1]) for c in peers]
     own0 = OB + V * rank
+
+    def col(c):
+        return T.ts[:, 16 * c + 15:16 * c + 16]
 
     def wblock(t, ph):
         return W[t][:, own0:own0 + V] if ph == 0 else W[t][:, 0:V]
@@ -116,326 +219,367 @@ def plan(g, core, T, topo, rank):
         ne = bin(mask).count("1")
         op("pool", fn, 500, r, [("arr", k)], prio, lat, sem=("ar%d" % k, ne * len(dsts), False, "sent%d" % k, ne))
 
-    for i in range(8):
-        e, q = (("sync", Yq), ("act", Cq))[i % 2]
-        op(e, lambda i=i, q=q: q.dma_start(T.pk[i::8, :], T.pts[i::16, 0:V]), 60, [], [("pk", i)], -110 + i, 2500, ("ldo", 128, True))
-    op("sync", lambda: Yq.dma_start(T.pi[:], T.pts[:, V:]), 60, [], ["piT"], -99.5, 3600, ("ldt", 16, True))
+    op("sync", lambda: Yq.dma_start(T.pi[:, 0:256], T.pts[:, 0:256]), 60, [], [("pi", 0)], -300, 2300, ("ldo", 16, True))
+    op("act", lambda: Cq.dma_start(T.pi[:, 256:V], T.pts[:, 256:V]), 60, [], [("pi", 1)], -500, 2500, ("ldp", 16, True))
     for j, (nm, a, b) in enumerate([("ld", 0, 64), ("cp", 64, 128), ("xs", 128, 160), ("ys", 160, 192)]):
-        op("act", lambda nm=nm, a=a, b=b: Cq.dma_start(T.li[:, a:b], T[nm][:]), 60, [], [("li", j)], -99 + j, 2200, ("ldl", 64, True))
+        op("sync", lambda nm=nm, a=a, b=b: Yq.dma_start(T.li[:, a:b], T[nm][:]), 60, [], [("li", j)], -298 + j, 3000, ("ldl", 64, True), [("pi", 0)])
+    op("sync", lambda: Yq.dma_start(T.pi[:, V:], T.pts[:, V:]), 60, [], [("pi", 2), ("pi", 3)], -290, 1400, ("ldt", 16, True), [("pi", 0)])
 
-    def sel(out, in_, pattern, fill, base, r, w, prio, n):
-        op("pool", lambda: g.affine_select(out, in_, pattern, A.not_equal, fill, base, -1), pool(n), r, w, prio)
-
-    def col(out, in0, s1, s2, o0, o1, r, w, prio):
-        if o1 is None:
-            op("dve", lambda: Vq.tensor_scalar(out, in0, s1, None, o0), dve(1), r, w, prio)
+    Z = T.zero
+    fill(Z[:], 0.0, XW // 2, ["zero"], -400)
+    sel(T.dx[:], Z[:, 0:128], [[16, 8], [0, 2], [1, 8]], 1.0, 0, ["zero"], ["dx"], -399, 128)
+    sel(T.du[:], Z[:, 0:128], [[16, 8], [-1000, 2], [1, 8]], -K / 512.0, 1000, ["zero"], ["du"], -398, 128)
+    op("pool", lambda: g.iota(T.mi[:], [[0, 16], [1, 16]], 128, -1), pool(256), ["ps"], ["mi"], -401)
+    ts(T.mj[:], T.mi[:], 15, None, A.bitwise_and, None, 256, ["mi"], ["mj"], -397)
+    ts(T.mk[:], T.mj[:], 0.0, None, A.is_equal, None, 256, ["mj"], ["mk"], -396)
+    if "paints" not in KEPT:
+        KEPT["paints"] = paints()
+    base, rest = KEPT["paints"]
+    for j, (a, b, st, val) in enumerate(base):
+        fill(T.tab[:, a:b:st], val, 64, [("tb", j)], -399)
+    for j, (a, b, st, val) in enumerate(rest):
+        n = len(range(a, b, st))
+        if j % 2:
+            fill(T.tab[:, a:b:st], val, n, [("tr", j)], -398, [("tb", x) for x in range(3)])
         else:
-            op("dve", lambda: Vq.tensor_scalar(out, in0, s1, s2, o0, o1), dve(1), r, w, prio)
-
-    q1 = T.qi[:, 0:1]
-    op("dve", lambda: Vq.memset(T.zero[:], 0.0), dve(512, .5), [], ["zero"], -100)
-    op("pool", lambda: g.iota(T.ki[:, 0:1], [[0, 1]], 0, 1), 140, [], ["ki"], -100)
-    op("pool", lambda: g.iota(T.jf[:, 0:4], [[1, 4]], 8, 0, allow_small_or_imprecise_dtypes=True), 140, [], ["jf"], -99)
-    col(q1, T.ki[:, 0:1], 15, None, A.bitwise_and, None, ["ki"], ["qi"], -99)
-    col(T.b14[:, 0:1], q1, 14.0, 2563.0, A.is_ge, A.mult, ["qi"], ["b14"], -98)
-    col(T.be[:, 0:1], T.b14[:, 0:1], -1.0, 2562.0, A.mult, A.add, ["b14"], ["be"], -97)
-    op("dve", lambda: Vq.tensor_copy(T.qf[:, 0:1], q1), dve(1), ["qi"], ["qf"], -75)
-    col(T.bo[:, 0:1], q1, 14.0, 2561.0, A.is_ge, A.mult, ["qi"], ["bo"], -72)
-    col(T.kp[:, 0:1], q1, 7.0, None, A.is_lt, None, ["qi"], ["kp"], -60)
-    col(T.bw0[:, 0:4], T.jf[:, 0:4], T.qf[:, 0:1], 2562.0, A.is_le, A.mult, ["jf", "qf"], ["bw0"], -59)
-    col(T.bw[:, 0:4], T.bw0[:, 0:4], T.b14[:, 0:1], None, A.subtract, None, ["bw0", "b14"], ["bw"], -58)
-    col(T.sw[:, 0:4], T.jf[:, 0:4], T.qf[:, 0:1], None, A.is_gt, None, ["jf", "qf"], ["sw"], -68)
-    col(T.bz0[:, 0:1], q1, 8.0, 2560.0, A.is_ge, A.mult, ["qi"], ["bz0"], -70)
-    col(T.bz[:, 0:1], T.bz0[:, 0:1], T.bo[:, 0:1], None, A.subtract, None, ["bz0", "bo"], ["bz"], -69)
-    op("dve", lambda: Vq.memset(T.h0[:], 0.0), dve(128, .5), [], [("h", 0, x) for x in range(4)], -61)
-    op("dve", lambda: Vq.memset(T.big[:], 4096.0), dve(32), [], ["big"], -57)
-    for j, (e, val) in enumerate(PATS):
-        rs = T["rs%d" % j]
-        op("dve", lambda rs=rs, e=e: Vq.memset(rs[:, 0:32 * e], -4.0), dve(32 * e, .5), [], [("rs", j)], -56 + j)
-        op("dve", lambda rs=rs, e=e, val=val: Vq.memset(rs[:, 0:32 * e:e], val), dve(32), [], [("rs", j)], -56 + j)
-    sel(T.pick[:], T.zero[:, 0:96], [[1, 12], [16, 8]], 1.0, 0, ["zero"], ["pick"], -98, 96)
-    sel(T.y0c[:], T.pick[:, 0:64], [[1, 8], [16, 8]], -8.0, 1, ["pick"], ["y0c"], -97, 64)
-    sel(T.y0c[:], T.y0c[:], [[0, 8], [16, 8]], 8.0, 9, ["y0c"], ["y0c"], -96, 64)
-    sel(T.ident[:], T.zero[:, 0:128], [[1, 128]], 1.0, 0, ["zero"], ["ident"], -95, 128)
-    sel(T.sh[:], T.zero[:, 0:128], [[1, 128]], 1.0, 8, ["zero"], ["sh"], -94.5, 128)
-    sel(T.selt[0:32, 0:512], T.zero[0:32, 0:512], [[1, 4], [4, 8], [0, 16]], 1.0, 0, ["zero"], ["selt0"], -94, 512)
-    sel(T.selt[0:32, 512:576], T.zero[0:32, 0:64], [[1, 32], [0, 2]], 1.0, 0, ["zero"], ["i20"], -80, 64)
-    sel(T.selt[0:32, 576:608], T.zero[0:32, 0:32], [[1, 32]], -1.0, 0, ["zero"], ["ni0"], -80, 32)
-    for j in range(1, 4):
-        op("sync", lambda j=j: Yq.dma_start(T.selt[32 * j:32 * j + 32, :], T.selt[0:32, :]), 60, ["selt0", "i20", "ni0"], [("rep", j)],
-           -50, 2000, ("rep", 48, True))
-    sel(T.yc[:, 8:96], T.pick[:, 8:96], [[1, 11], [16, 8]], -4096.0, 0, ["pick"], ["yc"], -79, 88)
-    sel(T.yc[:, 8:96], T.yc[:, 8:96], [[0, 11], [16, 8]], 4096.0, 14, ["yc"], ["yc"], -78, 88)
-    sel(T.yc[:, 8:96], T.yc[:, 8:96], [[0, 11], [16, 8]], -1.0, 15, ["yc"], ["yc"], -77, 88)
-    sel(T.yc[:, 0:8], T.pick[:, 0:8], [[16, 8]], -1.0, 15, ["pick"], ["ycb"], -76, 8)
-    for s in range(11):
-        sel(T.am[:, 144 * s:144 * s + 144], T.zero[:, 0:144], [[16, 9], [1000, 16]], 1.0, s - 15000, ["zero"], [("am", s)],
-            -70 + s if s < 8 else -40 + s, 144)
-    op("pool", lambda: g.iota(T.ownf[:], [[0, 64], [-128, 4]], -V * rank, -1, allow_small_or_imprecise_dtypes=True), pool(256), [], ["ownf"], -55)
-    sel(T.nid[:], T.zero[:, 0:128], [[1, 128]], -1.0, 0, ["zero"], ["nid"], -54, 128)
-    op("pool", lambda: g.affine_select(T.selw[:], T.selt[:, 0:512], [[0, 32], [32, 16]], A.is_ge, 0.0, -193, -1),
-       pool(512), ["selt0"] + [("rep", j) for j in range(1, 4)], ["selw"], -53)
-    op("act", lambda: Cq.activation(T.own[:], T.ownf[:], F.Identity), act(256), ["ownf"], ["own"], -5)
-    col(T.keep[:], T.ident[:], T.kp[:, 0:1], None, A.mult, None, ["ident", "kp"], ["keep"], -50)
+            ac(T.tab[:, a:b:st], Z[:, 0:n], F.Identity, n, ["zero"] + [("tb", x) for x in range(3)], [("tr", j)], -398, bias=val)
+    fill(T.tz[:], 1.0, 256, ["tz"], -395)
+    fill(T.tz[:, 0::16], 0.0, 16, ["tz"], -395)
+    tt(T.tm[:], T.tab[:], T.mk[:], A.mult, 256, ["mk"] + [("tr", j) for j in range(len(rest))], ["tm"], -394, 2)
+    scan(T.ts[:], T.tz[:], T.tm[:], A.mult, A.add, 256, ["tz", "tm"], ["col"], -393)
+    for par in range(2):
+        sg = 1.0 - 2 * par
+        sel(T.ws1[:, par::2], Z[:, 0:64], [[16, 8], [1000, 2], [2, 4]], -sg, 1 + par, ["zero"], [("ws", par)], -390, 64)
+        if par:
+            sel(T.ws1[:, 7::16], T.ws1[:, 7::16], [[16, 8]], 0.0, 8, [], [("ws", par)], -389, 8)
+        sel(T.ws1[:, par::2], T.ws1[:, par::2], [[16, 8], [1000, 2], [2, 4]], sg, 8 + par, [], [("ws", par)], -388, 64)
+    sel(T.ws1[:], T.ws1[:], [[16, 8], [1000, 2], [1, 8]], float(K), 0, [], [("ws", 0), ("ws", 1), "ws1"], -387, 128)
+    sel(T.ws0[:], T.ws1[:], [[16, 8], [-1000, 2], [1, 8]], 1.0, 1008, ["ws1"], ["ws0"], -386, 128)
+    sel(T.pick[:], Z[:, 0:64], [[16, 8], [-1, 8]], 1.0, 15, ["zero"], ["pick"], -385, 64)
+    iota(T.r0[:], [[0, 32], [4096, 8]], -1, 0, ["r0"], -384.9, 256)
+    sel(T.ident[:], Z[:, 0:128], [[1, 128]], 1.0, 0, ["zero"], ["ident"], -384.8, 128)
+    sel(T.sel[0:32, 0:512], Z[0:32, 0:512], [[1, 32], [0, 16]], 1.0, 0, ["zero"], ["selt"], -383, 512)
+    fill(T.one[:], 1.0, 8, ["one"], -396)
+    op("pool", lambda: g.affine_select(T.dg0[:], T.one[:], [[-16, 8]], A.is_ge, 0.0, 0, 1), pool(8), ["one", "ps"], ["dg0"], -384.7)
+    op("pool", lambda: g.affine_select(T.dg[:], T.dg0[:], [[16, 8]], A.is_ge, 0.0, 15, -1), pool(8), ["dg0", "ps"], ["dg"], -384.6)
     for t in range(RO):
-        for j, a in enumerate((EW, WW - 8)):
-            op("act", lambda t=t, a=a: Cq.activation(W[t][:, a:a + 8], T.zero[:, 0:8], F.Identity, bias=T.be[:, 0:1]), act(8),
-               ["zero", "be"], [("wE", t, j)], -90 + t)
-
-    def widen(src, r, parts, prio):
-        for h, bank, c0, eng, outs in parts:
-            mm([(T[bank][:, c0:c0 + 256], (T.ident, T.sh)[h][:], src, True, True, 128, 256)], r + ["ident", "sh", bank], [], prio)
-        for h, bank, c0, eng, outs in parts:
-            for out, n, key in outs:
-                if eng == "act":
-                    op("act", lambda out=out, bank=bank, n=n: Cq.activation(out, T[bank][:, 0:n], F.Identity, bias=T.bz[:, 0:1], scale=T.sw[:, 0:1]),
-                       act(n), ["bz", "sw"], [bank, key], prio)
-                else:
-                    op("dve", lambda out=out, bank=bank, n=n: Vq.tensor_scalar(out, T[bank][:, 0:n], T.sw[:, 0:1], T.bz[:, 0:1], A.mult, A.add),
-                       dve(n), ["bz", "sw"], [bank, key], prio)
-
-    op("dve", lambda: Vq.tensor_copy(T.k16[:], T.pk[:]), dve(256), [("pk", i) for i in range(8)], ["k16"], -200)
-    send(0, T.k16[:], T.land[:, 256 * rank:256 * rank + 256], ["k16"], -300, PAR["lat0"] - 1100)
-    op("dve", lambda: Vq.tensor_scalar(T.p16[:, V:], T.pi[:], T.be[:, 0:1], None, A.min), dve(512), ["piT", "be"], [("p16", 1)], -199)
-    widen(T.k16[:], ["k16"], [(0, "y1", 0, "act", []), (1, "y1", 256, "act", [(T.p16[:, 0:V], 512, ("p16", 0))])], -198)
+        for x in range(2):
+            ev(("act", "dve")[x], T.sp[:, 16 * t + 8 * x:16 * t + 8 * x + 8], T.dg[:], 8, ["dg", "col"], [("sp", t, x)], -196 + t, col(4 * x + t))
+    fill(T.pen[:, :, :], 0.0, 128, [("pen", t) for t in range(RO)], -60)
+    for s in range(8):
+        sel(T.am[:, 144 * s:144 * s + 144], Z[:, 0:144], [[16, 9], [1000, 16]], 1.0, 8 + s - 15000, ["zero"], [("am", s)], -190 + s, 144)
+    sel(T.pick9[:], Z[:, 0:72], [[16, 8], [-1, 9]], 1.0, 16, ["zero"], ["pick9"], -182, 72)
+    sel(T.pick9[:], T.pick9[:], [[16, 8], [0, 9]], -1.0, 0, [], ["pick9"], -182, 72)
+    sel(T.pick9[:, 0::9], Z[:, 0:8], [[16, 8]], 2560.0, 0, [], ["pick9"], -182, 8)
+    iota(T.own[:], [[-128, 4], [0, 64]], -V * rank, 0, ["own"], -180, 256)
+    iota(T.ownf[:, 0:1], [[0, 1]], 0, -1, ["ownf"], -180, 1)
+    for nm, val, pr in (("nid", -1.0, -175), ("nkd", -KD, -171)):
+        sel(T[nm][:], Z[:, 0:128], [[1, 128]], val, 0, ["zero"], [nm], pr, 128)
+    for c in range(4):
+        sel(T.seld[0:32, 8 * c:8 * c + 8, :], Z[0:32, 0:XW], [[1, 8], [0, NX * L]], KD, 8 * c, ["zero"], [("seld", c)], -170 + c, XW)
+    sel(T.sel[0:32, SN:SW], Z[0:32, 0:32], [[1, 32]], -1.0, 0, ["zero"], ["ni"], -160, 32)
+    s0k = ["selt", "ni"] + [("seld", c) for c in range(4)]
+    for j in range(1, 4):
+        op("sync", lambda j=j: Yq.dma_start(T.sel[32 * j:32 * j + 32, :], T.sel[0:32, :]), 60, s0k, [("rep", j)], -50, 2500, ("rep", 96, True))
+        op("sync", lambda j=j: Yq.dma_start(T.seld[32 * j:32 * j + 32, :, :], T.seld[0:32, :, :]), 60, s0k, [("rep", j + 3)], -50, 2500, ("rep", 96, True))
+    rep = [("rep", j) for j in range(1, 7)]
+    ac(T.selw[:], Z[:, 0:512], F.Identity, 512, ["zero"], ["selw0"], -98)
+    swk = []
+    for r in (8, 13, 14, 15):
+        swk.append(("selw", r))
+        sel(T.selw[:, r::16], T.sel[:, r:512:16], [[0, 32]], 0.0, 1000, ["selw0", "selt"] + rep, [swk[-1]], -40, 32)
+    fill(T.h0[:], 0.0, 64, [("h", 0, x) for x in range(4)], -390)
+    for e in sorted(set(NPS) | set(10 + t - ph - NPS[ph] for t in range(RO) for ph in range(2))):
+        iota(T["rs%d" % e][:, 0:32 * e], [[0, 32], [-4096, e]], 2560, 0, [("rs", e)], -170 + 5 * e, 32 * e)
+    for r, ws in ((9, [1]), (10, [K, -1]), (11, [K, K, 1]), (12, [K, K, K, -1])):
+        for j, val in enumerate(ws):
+            swk.append(("selw", r, j))
+            sel(T.selw[32 * j:32 * j + 32, r::16], Z[32 * j:32 * j + 32, 0:32], [[1, 32]], float(val), 0, ["selw0"], [swk[-1]] + ["ps"] * (j > 0), -45 + j, 32)
     for ph in range(2):
-        op("act", lambda ph=ph: Cq.activation(wblock(0, ph), T.p16[:, V * ph:V * ph + V], F.Identity), act(512), [("p16", ph)], [("w", 0, ph)], -30 + ph)
-    op("act", lambda: Cq.activation(T.out0[:], T.p16[:], F.Identity, bias=T.bo[:, 0:1]), act(1024), [("p16", 0), ("p16", 1), "bo"], ["out0"], -4)
+        n = 64 * NPS[ph]
+        sel(XM[ph][:, 0:n // 2, 0:2], Z[:, 0:n], [[0, n]], 2560.0, 0, ["zero"], [("xm", ph, c) for c in range(4)], -20, n, 0)
+
+    def copy(out, in_, r, w, prio, n):
+        sel(out, in_, [[0, n]], 0.0, 1000, r, w, prio, n)
+
+    def build(j, out, st, hist, r, w, prio, eng, n=V):
+        b = bank("*")
+        src = cols(b, 0, n)
+        grp = [(src, (T.ws1, T.ws0)[j == 0][:], st, True, hist is None, 128, n)]
+        if hist is not None:
+            grp += [(cols(b, 128 * c, 128), T.selw[0:32 * j + 32, 128 * c:128 * c + 128], hist, False, c == 3, 128, 128) for c in range(4)]
+            r = r + swk
+        mm(grp, r + ["ws0", "ws1", b], [], prio)
+        for o, k in zip(out, w):
+            ev(eng, o, src, n, ["col"], [b, k], prio, col(14) if j else 1.0, col(13 if j else 12))
+
+    for ph in range(2):
+        a, pr = V * ph, -350 + 100 * ph
+        for c0, n in ((0, 256), (256, 256)) if ph == 0 else ((V, V),):
+            ks = range(c0 // 256, (c0 + n) // 256)
+            ts(T.x16[:, c0:c0 + n], T.pi[:, c0:c0 + n], 2048.0, None, A.min, None, n, [("pi", x) for x in ks], [("x16", x) for x in ks], pr)
+            ac(T.u16[:, c0:c0 + n], T.pi[:, c0:c0 + n], F.Relu, n, [("pi", x) for x in ks], [("u16", x) for x in ks], pr, bias=-2048.0)
+        for hf in range(2):
+            c0, b = a + 256 * hf, bank("*")
+            mm([(cols(b, 0, 256), T.dx[:], T.x16[:, c0:c0 + 256], True, False, 128, 256),
+                (cols(b, 0, 256), T.du[:], T.u16[:, c0:c0 + 256], False, True, 128, 256)],
+               [("x16", 2 * ph + hf), ("u16", 2 * ph + hf), "dx", "du", b], [], pr + 1)
+            ev(("act", "dve")[hf], T.pq[:, c0:c0 + 256], cols(b, 0, 256), 256, [], [b, ("pq", ph, hf)], pr + 2)
+        if ph == 0:
+            send(0, T.pq[:, 0:V], T.land[:, V * rank:V * rank + V], [("pq", 0, 0), ("pq", 0, 1)], -500, PAR["lat0"])
+    pqk = [[("pq", ph, 0), ("pq", ph, 1)] for ph in range(2)]
+    ts(T.lt[:], T.li[:], 2048.0, -2568.0, A.is_ge, A.mult, 192, [("li", j) for j in range(4)], ["lt"], -145)
+    tt(T.lu[:], T.lt[:], T.li[:], A.add, 192, ["lt"], ["lu"], -144, 2)
+    ts(T.lo[:], T.lu[:], float(OB), None, A.add, None, 192, ["lu"], ["lo"], -143)
+
+    def hk(ph, j):
+        return [("h", ph, x) for x in range(j + 1)] + s0k[:2] + (rep if j else [])
+
+    for ph in range(2):
+        pr = -240 + 10 * ph
+        build(0, [wblock(0, ph)], T.pq[:, V * ph:V * ph + V], None, pqk[ph], [("w", 0, ph)], pr + 3, ("dve", "act")[ph])
+        b, b2, b3 = bank("d"), bank("*"), bank("*")
+        mm([(B(b)[:, 64 * c:64 * c + 64], T.pq[:, V * ph + 128 * c:V * ph + 128 * c + 128], T.pick[:], True, True, 128, 64) for c in range(4)],
+           pqk[ph] + ["pick", b], [], pr)
+        scan(T.t0[:, 256 * ph:256 * ph + 256], T.r0[:], B(b)[:, 0:256], A.min, A.max, 256, ["r0"], [b, ("t0", ph)], pr)
+        mm([(cols(b2, 0, 128, 0, 32), T.t0[:, 256 * ph + 7:256 * ph + 256:8], T.ident[:], True, True, 32, 128)], [("t0", ph), "ident", b2], [], pr)
+        ev("dve", H[ph][0:32, :], cols(b2, 0, 128, 0, 32), 128, [], [b2, ("h", ph, 0)], pr, 1.0, 1.0)
+        mm([(cols(b3, 128 * c, 128), T.sel[0:32, 128 * c:128 * c + 128], H[ph][0:32, :], True, True, 128, 128) for c in range(4)],
+           [("h", ph, 0), "selt", b3], [], pr + 1)
+        ev("act", T.top[:, V * ph:V * ph + V], cols(b3, 0, V), V, ["col"], [b3, ("top", ph)], pr + 1, col(8), col(9))
+    ac(T.e16[:], Z[:, 0:8], F.Identity, 8, ["zero", "col"], ["e16"], -235, bias=col(15))
+    build(0, [W[0][:, EW:OB]], T.e16[:], None, ["e16"], [("wE", 0)], -234, "act", 8)
+    build(1, [W[t][:, EW:OB] for t in range(1, RO)], T.e16[:], None, ["e16"], [("wE", t) for t in range(1, RO)], -233, "act", 8)
+    ac(T.out0[:], T.pi[:], F.Identity, 1024, [("pi", x) for x in range(4)], ["out0"], -97)
     op("sync", lambda: Yq.dma_start(T.yp[:], T.out0[:]), 60, ["out0"], ["yp0"], -4, 3000, ("o0", 16, True))
-    op("dve", lambda: Vq.tensor_scalar(T.lt[:], T.li[:], 2048.0, -2568.0, A.is_ge, A.mult), dve(192), [("li", j) for j in range(4)], ["lt"], -145.5)
-    op("dve", lambda: Vq.tensor_tensor(T.lu[:], T.lt[:], T.li[:], A.add), dve(192, 2), ["lt"], ["lu"], -44)
-    op("dve", lambda: Vq.tensor_scalar(T.lo[:], T.lu[:], float(OB), None, A.add), dve(192), ["lu"], ["lo"], -43)
-    mm([(T.y0[:, 2 * c + ph:512:8], T.p16[:, V * ph + 128 * c:V * ph + 128 * c + 128], T.y0c[:], True, True, 128, 64)
-        for ph in range(2) for c in range(4)], [("p16", 0), ("p16", 1), "y0c", "y0"], [], -150)
-    op("dve", lambda: Vq.tensor_copy(T.t1[:], T.y0[:, 256:512]), dve(256), [], ["y0", "t1"], -149)
-    op("dve", lambda: Vq.tensor_tensor(T.t2[:], T.y0[:, 0:256], T.t1[:], A.min), dve(256), ["t1"], ["y0", "t2"], -148)
-    op("dve", lambda: Vq.tensor_tensor(T.t3[:], T.t2[:, 0:128], T.t2[:, 128:256], A.min), dve(128, 2), ["t2"], ["t3"], -147)
-    op("dve", lambda: Vq.tensor_tensor(T.a0[:], T.t3[:, 0:64], T.t3[:, 64:128], A.min), dve(64, 2), ["t3"], ["a0"], -146)
-    op("dve", lambda: Vq.tensor_scalar(T.u0[:], T.a0[:], 2304.0, -4864.0, A.is_ge, A.mult), dve(64), ["a0"], ["u0"], -145)
-    mm([x for ph in range(2) for x in (
-        (T.m1[0:32, 128 * ph:128 * ph + 128], T.a0[:, ph::2], T.ident[:], True, False, 32, 128),
-        (T.m1[0:32, 128 * ph:128 * ph + 128], T.u0[:, ph::2], T.ident[:], False, True, 32, 128))],
-       ["a0", "u0", "ident", "m1"], [], -144)
-    for ph in range(2):
-        op("dve", lambda ph=ph: Vq.tensor_scalar(H[ph][0:32, :], T.m1[0:32, 128 * ph:128 * ph + 128], -1.0, None, A.max),
-           dve(128), [], ["m1", ("h", ph, 0)], -143 + ph)
-
-    def tcol(t, ph):
-        n = 2 * t + ph
-        return T.top[:, V * n:V * n + V]
-
-    def hkeys(ph, j):
-        return [("h", ph, x) for x in range(j + 1)] + ["selt0", "i20", "ni0"] + [("rep", x) for x in range(1, j + 1)]
-
-    def build_block(j, out, st, hist, r, w, bank, prio, eng):
-        mm([(T[bank][:], T.keep[:], st, True, False, 128, 512)] +
-           [(T[bank][:, 128 * c:128 * c + 128], T.selw[0:32 * j + 32, 128 * c:128 * c + 128], hist, False, c == 3, 128, 128)
-            for c in range(4)], r + ["keep", bank, "selw"], [], prio)
-        if eng == "act":
-            op("act", lambda: Cq.activation(out, T[bank][:], F.Identity, bias=T.bw[:, j:j + 1], scale=T.sw[:, j:j + 1]), act(512),
-               ["bw", "sw"], [bank, w], prio)
-        else:
-            op("dve", lambda: Vq.tensor_scalar(out, T[bank][:], T.sw[:, j:j + 1], T.bw[:, j:j + 1], A.mult, A.add), dve(512),
-               ["bw", "sw"], [bank, w], prio)
-
-    def build_top(j, ph, bank, prio):
-        mm([(T[bank][:, 128 * c:128 * c + 128], T.selt[0:32 * j + 32, 128 * c:128 * c + 128], H[ph][0:32 * j + 32, :], True, True, 128, 128)
-            for c in range(4)], hkeys(ph, j)[:j + 2] + [("rep", x) for x in range(1, j + 1)] + [bank], [], prio)
-        op("act", lambda: Cq.activation(tcol(j, ph), T[bank][:], F.Identity), act(512), [], [bank, ("top", j, ph)], prio)
-
-    for ph, bank in enumerate(("m2", "m3")):
-        build_top(0, ph, bank, -140 + ph)
-        op("dve", lambda ph=ph, bank=bank: Vq.tensor_tensor(T.sc[:, V * ph:V * ph + V], T[bank][:], T.p16[:, V * ph:V * ph + V], A.min),
-           dve(512), [("p16", ph)], [bank, ("sc", ph)], -42 + ph)
-    send(4, T.sc[:, 0:V], T.scl[:, V * rank:V * rank + V], [("sc", 0)], -60.5, PAR["lat0"])
-    qa, qb, qc = others
-
-    def wq(q, a, b):
-        return T.w0[:, OB + V * q + a:OB + V * q + b]
-
-    def lq(q):
-        return T.land[:, 256 * q:256 * q + 256]
-
-    widen(lq(qa), [("arr", 0)], [(0, "y1", 0, "act", []), (1, "y1", 256, "act", [(wq(qa, 0, V), 512, ("wr", 0))])], -252)
-    widen(lq(qb), [("arr", 0)], [(0, "y2", 0, "dve", []), (1, "y2", 256, "dve", [(wq(qb, 0, V), 512, ("wr", 1))])], -251)
-    widen(lq(qc), [("arr", 0)], [(0, "q0", 0, "act", [(wq(qc, 0, 256), 256, ("wr", 2))]), (1, "q1", 0, "dve", [(wq(qc, 256, V), 256, ("wr", 3))])], -250)
+    for x, q in enumerate(others):
+        for a, n, e in ((0, V, ("act", "dve")[x]),) if x < 2 else ((0, 256, "act"), (256, 256, "dve")):
+            c0 = V * q + a
+            build(0, [W[0][:, OB + c0:OB + c0 + n]], T.land[:, c0:c0 + n], None, [("arr", 0)], [("wq", 0, x + a // 256)], -20 + x, e, n)
 
     def wkeys(t, full):
-        k = [("w", t, 0), ("wE", t, 0), ("wE", t, 1)]
-        k += [("wr", j) for j in range(4)] if t == 0 else [("wq", t, x) for x in range(NR - 1)]
-        return k + ([("w", t, 1)] if full else [])
+        return [("wq", t, x) for x in range(NR)] + [("w", t, 0), ("wE", t)] + ([("w", t, 1)] if full else [])
 
-    def lists(t, edges, c0, n, bank, prio):
+    def lists(t, s, row, phs, prio):
+        b, c0, n = bank("*"), 32 * phs[0], 32 * len(phs)
+        mm([(cols(b, 0, n), T.am[:, 144 * row + 15 - r:144 * row + 143 - r], T.xl[:, 1024 * t + 16 * c0 + r:1024 * t + 16 * (c0 + n):16],
+             r == 0, r == 15, 128, n) for r in range(16)], [("xl", t, p) for p in phs] + [("am", row), b], [], prio)
+        ac(T.eo[:, phs[0]:phs[-1] + 1, 32 * s:32 * s + 32], cols(b, 0, n), F.Relu, n, [], [b] + [("eo", s, p) for p in phs], prio, bias=8.0)
+
+    def leave(t, ph, po):
+        lo, hi = (0, 96) if t < RO - 1 else (96, 128)
+        b = bank("*")
         grp = []
-        for i, s in enumerate(edges):
-            for r in range(16):
-                a = 1024 * t + 16 * c0 + r
-                grp.append((T[bank][:, n * i:n * i + n], T.am[:, 144 * s + 15 - r:144 * s + 143 - r], T.xl[:, a:1024 * t + 16 * (c0 + n):16],
-                            r == 0, r == 15, 128, n))
-        phs = [0, 1] if n == 64 else [c0 // 32]
-        mm(grp, [("xl", t, p) for p in phs] + [("am", s) for s in edges] + [bank], [], prio)
-        e0 = 64 * edges[0] + c0
-        op("dve", lambda: Vq.tensor_scalar(T.eo[:, e0:e0 + n * len(edges)], T[bank][:, 0:n * len(edges)], 8.0, 2056.0, A.add, A.min),
-           dve(n * len(edges)), [], [bank] + [("eo", s, p) for s in edges for p in phs], prio)
+        for x in range(lo, hi, 32):
+            grp.append((cols(b, 0, 128, x, x + 32), T.aa[:, 128 * ph + x:128 * ph + x + 32], T.ident[:], True, x > 0, 32, 128))
+            if x == 0:
+                grp.append((cols(b, 0, 128, 0, 32), T.u[:, 128 * ph:128 * ph + 32], T.nid[:], False, True, 32, 128))
+        mm(grp, [("aa", 2 * y + ph) for y in range(lo // 32, hi // 32)] + [("u", ph), "ident", "nid", b], [], po)
+        ac(T.go[lo:hi, 128 * ph:128 * ph + 128], cols(b, 0, 128, lo, hi), F.Abs, 128, [], [b, ("go", t, ph)], po)
+        for c in range(lo // 8, hi // 8):
+            e, q = ("act", Cq) if lo and ph and c % 2 else ("sync", Yq)
+            a = V * ph + 128 * (c % 4)
+            op(e, lambda q=q, c=c, a=a: q.dma_start(T.yp[8 + c // 4::16, a:a + 128], T.go[8 * c:8 * c + 8, 128 * ph:128 * ph + 128]),
+               PAR["dq"], [("go", t, ph), "yp0"], [("yp", ph, c)], po, 2000, ("outs", 16 * 8 * RO, True))
 
-    def load_sets(t, ph, prio):
-        op("act", lambda: Cq.activation(T.xl[:, 1024 * t + V * ph:1024 * t + V * ph + V], W[t][:].indirect(T.lo[:, 32 * ph:32 * ph + 32]), F.Identity),
-           act(512, GA), wkeys(t, True) + ["lo"], [("xl", t, ph)], prio)
+    def plain(eng, out, win, gs, r, w, prio):
+        if eng == "a":
+            ac(out, win, F.Identity, V, r, w, prio, GA, scale=gs)
+        else:
+            ts(out, win, gs, None, A.mult, None, V, r, w, prio, GA)
 
-    cnt = dict(m=0, y=1, z=0)
+    def xpart(t, ph, c):
+        w = 8 * NPS[ph] * XL[t]
+        return XT[ph][:, XO[t] + w * c:XO[t] + w * c + w]
+
+    def kept(t, ph, p0):
+        n, kk, lt, NP = 2 * t + ph, 32 * t + 32, XL[t], NPS[ph]
+        m = -(-32 // min(8, 512 // (NP * lt)))
+        cuts = [32 * x // m for x in range(m + 1)]
+        for c in range(m):
+            d = bank("d")
+            a, b = cuts[c], cuts[c + 1]
+            xw = (b - a) * NP * lt
+            xs, ro, pr = XT[ph][:, XO[t] + a * NP * lt:XO[t] + b * NP * lt], RS[ph][:, a * NP * lt:b * NP * lt], p0 + .1 * c
+            xk = [("xt", t if t > 1 else 0, ph, x) for x in range(a // 8, (b + 7) // 8)]
+            mm([(B(d)[:, 0:xw], T.nkd[:], xs, True, False, 128, xw),
+                (B(d)[:, 0:xw], H[ph][0:kk, :], T.seld[0:kk, a:b, 0:NP * lt], False, True, 128, xw)],
+               xk + ["nkd", d] + [("seld", x) for x in range(a // 8, (b + 7) // 8)] + hk(ph, t), [], pr)
+            if c < PAR["ob"][n]:
+                db = T.db[:, 512 * (c % 2):512 * (c % 2) + xw]
+                ac(db, B(d)[:, 0:xw], F.Identity, xw, [], [d, ("db", c % 2)], pr)
+                scan(ro, db, xs, A.min, A.max, xw / 2, xk + [("db", c % 2), ("ro", ph)], [("ro", n, c)], pr)
+            else:
+                scan(ro, B(d)[:, 0:xw], xs, A.min, A.max, xw, xk + [("ro", ph)], [d, ("ro", n, c)], pr)
+        scan(T.sr[:, GW * n:GW * n + 32 * NP], T["rs%d" % NP][:, 0:32 * NP], RS[ph][:, lt - 1:32 * NP * lt:lt], A.max, A.min, 16 * NP,
+             [("rs", NP)], [("ro", ph), ("sr", n)], p0 + .4)
+
     for t in range(RO):
-        R = 9 + t
+        gs = col(11 if t else 10)
+        fk = wkeys(t, True) + ["lo", "col"]
         if t == 0:
             for ph in range(2):
-                load_sets(0, ph, -3 + .1 * ph)
-            lists(0, [0], 0, 32, "m2", -2)
-            for edges, bank, pr in (([1], "m3", -1.9), ([2, 3], "m1", -1.89), ([4, 5], "m2", .01), ([6, 7], "m3", .11)):
-                lists(0, edges, 0, 64, bank, pr)
-            lists(0, [0], 32, 32, "m1", .3)
-        else:
-            for ph in range(2):
-                pr = 2 * t - 0.06 if ph == 0 else 2 * t + PAR["ldt"]
-                load_sets(t, ph, pr)
-                lists(t, [7 + t], 32 * ph, 32, "m2", pr)
-        s0, P = (0, 8) if t == 0 else (7 + t, 1)
-        pr = 2 * t - 0.05
-        op("act", lambda t=t: Cq.activation(T.xx[:, V * t:V * t + V], W[t][:].indirect(T.lo[:, 128:160]), F.Identity), act(512, GA),
-           wkeys(t, True) + ["lo"], [("xx", t)], pr)
-        mm([(T.m3[:, 0:32 * P], T.ident[:], T.own[:, 0:32 * P], True, False, 128, 32 * P)] +
-           [(T.m3[:, c:32 * P:4], T.xx[:, V * t + 128 * c:V * t + 128 * c + 128], T.pick[:, 8 * s0:8 * (s0 + P)], False, c == 3, 128, 8 * P)
-            for c in range(4)], [("xx", t), "own", "ident", "pick", "m3"], [], pr)
-        op("act", lambda P=P: Cq.activation(T.ab[:, 0:32 * P], T.m3[:, 0:32 * P], F.Abs), act(32 * P), [], ["m3", "ab"], pr)
-        op("act", lambda P=P, s0=s0: Cq.activation(T.zx[:, 32 * s0:32 * (s0 + P)], T.ab[:, 0:32 * P], F.Relu, bias=4096.0, scale=-4096.0),
-           act(32 * P), ["ab"], [("zx", t)], pr)
-        mm([(T.m3[:, 256:288], T.ident[:], T.zx[:, 32 * p:32 * p + 32], p == 0, p == 7 + t, 128, 32) for p in range(8 + t)],
-           [("zx", x) for x in range(t + 1)] + ["ident", "m3"], [], pr)
-        op("act", lambda t=t: Cq.activation(T.pen[:, 32 * t:32 * t + 32], T.m3[:, 256:288], F.Relu, bias=4096.0, scale=-1.0),
-           act(32), [], ["m3", ("pen", t)], pr)
-
+                plain("ad"[ph], T.xl[:, V * ph:V * ph + V], W[0][:].indirect(T.lo[:, 32 * ph:32 * ph + 32]), gs, fk, [("xl", 0, ph)], -3)
+            for s in range(8):
+                lists(0, s, s, [0, 1], -2 + .1 * s)
         for ph in range(2):
             n = 2 * t + ph
-            old = list(range(8 if t == 0 else 7 + t))
-            places = ["cp", "ys"] if ph == 0 else ["cp"]
+            kk, NP = 32 * t + 32, NPS[ph]
+            for s in PAR["rd"][n]:
+                ts(RAW[ph][:, V * s:V * s + V], W[t][:, EW:WW].indirect(T.eo[:, ph, 32 * s:32 * s + 32]), gs, 0.0 if t else 1.0, A.mult, A.add, V,
+                   wkeys(t, False) + [("eo", s, ph), "col"], [("raw", ph, s)], n - .4, GA)
+            for grp in PAR["rg"][ph]:
+                grp = [s for s in grp if s not in PAR["rd"][n]]
+                if not grp:
+                    continue
+                a, b = grp[0], grp[-1] + 1
+                ac(RAW[ph][:, V * a:V * b], W[t][:, EW:WW].indirect(T.eo[:, ph, 32 * a:32 * b]), F.Identity, V * (b - a),
+                   wkeys(t, False) + [("eo", s, ph) for s in grp] + ["col"], [("raw", ph, s) for s in grp], n - .5 + .02 * a, GA,
+                   scale=gs, bias=0.0 if t else 1.0)
+            rk = [("raw", ph, s) for s in range(NP)] + ["pick"]
+
+            def piece(k, c):
+                return RAW[ph][:, V * k + 128 * c:V * k + 128 * c + 128]
+
+            gt, sr = T.gt[:, GW * n:GW * n + 32 * NP], T.sr[:, GW * n + NP - 1:GW * n + 32 * NP:NP]
             if t == 0:
-                order = ["cp"] + old[:5] + places[1:] + old[5:]
-                first = {"cp": -0.5, "ys": -0.45} if ph == 0 else {}
+                for c in range(4):
+                    b = bank()
+                    mm([(B(b)[:, :, 9 * k:9 * k + 9], piece(k, c), T.pick9[:], True, True, 128, 72) for k in range(NP)], rk + ["pick9", b], [], n + .2 + .05 * c)
+                    ev(PAR["x0"][c], xpart(0, ph, c), B(b)[:, :, 0:NP * 9], 72 * NP, [], [b, ("xt", 0, ph, c)], n + .2 + .05 * c)
+                    copy(XM[ph][:, 8 * NP * c:8 * NP * (c + 1), 2:L], xpart(0, ph, c), [("xt", 0, ph, c)], [("xm", ph, c)], n + 1.5, 72 * NP)
+                kept(0, ph, n + .3)
             else:
-                order = old + places + [7 + t]
-                first = {}
+                b, b2 = bank(), bank()
+                mm([(B(b)[:, c, k:8 * NP:NP], piece(k, c), T.pick[:, 7::8], True, True, 128, 8) for k in range(NP) for c in range(4)],
+                   rk + [b], [], n + .1)
+                ac(gt, B(b)[:, 0:4, 0:8 * NP], F.Identity, 32 * NP, [], [b, ("gt", n)], n + .1)
+                mm([(B(b2)[:, 0:4, 0:8 * NP], T.nkd[:], gt, True, False, 128, 32 * NP),
+                    (B(b2)[:, 0:4, 0:8 * NP], H[ph][0:kk, :], T.seld[0:kk, :, 0:NP], False, True, 128, 32 * NP)],
+                   [("gt", n), "nkd", b2] + hk(ph, t), [], n + .2)
+                zb = T.zb[:, GW * ph:GW * ph + 32 * NP]
+                tt(zb, B(b2)[:, 0:4, 0:8 * NP], gt, A.max, 32 * NP, [("gt", n)], [b2, ("zb", ph)], n + .2)
+                scan(T.zs[:, GW * n:GW * n + 32 * NP], T["rs%d" % NP][:, 0:32 * NP], zb, A.max, A.min, 32 * NP, [("zb", ph), ("rs", NP)], [("zs", n)], n + .2)
+                tt(T.a1[:, 32 * n:32 * n + 32], T.zs[:, GW * n + NP - 1:GW * n + 32 * NP:NP], sr, A.min, 64, [("zs", n), ("sr", n)], [("a1", n)], n + .3)
+                if t < RO - 1:
+                    copy(XM[ph][:, 0:32 * NP, 3 - t], gt, [("gt", n)], [("xm", ph, c) for c in range(4)], n + .4, 32 * NP)
+                    for c in range(4):
+                        copy(xpart(t + 1, ph, c), XM[ph][:, 8 * NP * c:8 * NP * (c + 1), 2 - t:L], [("xm", ph, c)], [("xt", t + 1, ph, c)],
+                             n + .5, 8 * NP * XL[t + 1])
+                a = 1024 * t + V * ph
+                plain(PAR["lde"][n], T.xl[:, a:a + V], W[t][:].indirect(T.lo[:, 32 * ph:32 * ph + 32]), gs, fk, [("xl", t, ph)], n - .3)
+                lists(t, 7 + t, 0, [ph], n - .3)
+            if ph == 0:
+                P, pr, b, b2 = 8 if t == 0 else 1, n - .2, bank(), bank("*")
+                z0 = 0 if t == 0 else 224 + 32 * t
+                plain(PAR["xse"][t], T.xx[:, V * t:V * t + V], W[t][:].indirect(T.lo[:, 128:160]), gs, fk, [("xx", t)], pr)
+                mm([(B(b)[:, 0:4, 0:8 * P], T.ident[:], T.own[:, ::8 // P], True, False, 128, 32 * P)] +
+                   [(B(b)[:, c, 0:8 * P], T.xx[:, V * t + 128 * c:V * t + 128 * c + 128], T.pick[:, 8 // P - 1::8 // P], False, c == 3, 128, 8 * P)
+                    for c in range(4)], [("xx", t), "own", "ident", "pick", b], [], pr)
+                ac(T.ab[:, 0:32 * P], B(b)[:, 0:4, 0:8 * P], F.Abs, 32 * P, ["ownf"], [b, "ab"], pr, bias=T.ownf[:, 0:1])
+                ac(T.zx[:, z0:z0 + 32 * P], T.ab[:, 0:32 * P], F.Relu, 32 * P, ["ab"], [("zx", t)], pr, bias=4096.0, scale=-4096.0)
+                grp = [(cols(b2, 0, 32), T.nid[:], T.zx[:, z0 + p:z0 + 32 * P:P], p == 0, t == 0 and p == P - 1, 128, 32) for p in range(P)]
+                if t:
+                    grp.append((cols(b2, 0, 32), T.ident[:], T.pen[:, 4 * t - 4:4 * t, 0:8], False, True, 128, 32))
+                mm(grp, [("zx", t), ("pen", t - 1), "ident", "nid", b2], [], pr)
+                ac(T.pen[:, 4 * t:4 * t + 4, 0:8], cols(b2, 0, 32), F.Relu, 32, [], [b2, ("pen", t)], pr, bias=0.0 if t else 4096.0)
+            if ph == 1 and t < RO - 1:
+                for x, q in enumerate(others):
+                    a = 512 * t + 128 * q
+                    build(t + 1, [W[t + 1][:, OB + V * q:OB + V * q + V]], T.land[:, V * q:V * q + V], T.hl[0:kk + 32, a:a + 128],
+                          [("arr", t + 1), ("arr", 0)], [("wq", t + 1, x)], n - .1, PAR["rem"][t][x])
+            if t == RO - 1:
+                leave(t - 1, ph, n + .5)
+            places = ["cp", "ys"] if ph == 0 else ["cp"]
+            order = places + list(range(NP, 8)) if t == 0 else list(range(NP, 7 + t)) + places + [7 + t]
             E = len(order)
-            Ep = E + E % 2
-            pat = PATS.index((Ep, 2560.0 if t == RO - 1 else 2304.0))
             Q = "q%d" % ph
-            half = Ep // 2
-            for gi in range(half):
-                srcs = order[2 * gi:2 * gi + 2]
-                zs = cnt["z"] % ZS
-                cnt["z"] += 1
-                zb = ZW * zs
-                for si, s in enumerate(srcs):
-                    pr = n + (2 * gi + si) / 20.0
-                    mi = cnt["m"]
-                    cnt["m"] += 1
-                    mt = T.m[:, 512 * mi:512 * mi + 512]
-                    if s == "cp":
-                        win, off, rk = W[t][:], T.lo[:, 64 + 32 * ph:96 + 32 * ph], wkeys(t, True) + ["lo"]
-                    elif s == "ys":
-                        win, off, rk = W[t][:], T.lo[:, 160:192], wkeys(t, True) + ["lo"]
-                    else:
-                        win, off, rk = W[t][:, EW:WW], T.eo[:, 64 * s + 32 * ph:64 * s + 32 * ph + 32], wkeys(t, False) + [("eo", s, ph)]
-                    op("dve", lambda mt=mt, win=win, off=off, t=t, ph=ph: Vq.tensor_tensor(mt, win.indirect(off), tcol(t, ph), A.max),
-                       dve(512, GA), rk + [("top", t, ph)], [("m", mi)], first.get(s, pr))
-                    yb = Y[cnt["y"] % 3]
-                    cnt["y"] += 1
-                    mm([(T[yb][:, c:32 * R:4], T.m[:, 512 * mi + 128 * c:512 * mi + 128 * c + 128], T.yc[:, 0:8 * R], True, True, 128, 8 * R)
-                        for c in range(4)], [("m", mi), "yc", "ycb", yb], [], pr)
-                    op("act", lambda yb=yb, zb=zb, si=si, R=R: Cq.activation(T.z[:, zb + si:zb + 64 * R:2], T[yb][:, 0:32 * R], F.Relu),
-                       act(32 * R), [], [yb, ("z", zs, si)], pr)
-                G = len(srcs)
-                st = 2 // G
-                qo = T[Q][:, gi:32 * Ep:half * st]
-                grp = [(qo, H[ph][0:32 * t + 32, :], T.selt[0:32 * t + 32, 512:576:st], True, False, 128, 32 * G)]
-                rk = hkeys(ph, t) + ["ident", Q] + [("z", zs, si) for si in range(G)]
-                if "ys" in srcs:
-                    a = gi + half * srcs.index("ys")
-                    grp.append((T[Q][:, a:32 * Ep:Ep], T.ident[:], T.pen[:, 32 * t:32 * t + 32], False, False, 128, 32))
-                    rk.append(("pen", t))
-                grp += [(qo, T.ident[:], T.z[:, zb + 64 * p:zb + 64 * p + 64:st], False, p == R - 1, 128, 32 * G) for p in range(R)]
-                if G == 1:
-                    grp.append((T[Q][:, gi + half:32 * Ep:Ep], T.ident[:], T.big[:], True, True, 128, 32))
-                    rk.append("big")
-                mm(grp, rk, [], n + (2 * gi + 1.5) / 20.0)
-            pr = n + 0.9
-            so = T.so[:, 448 * n:448 * n + 32 * Ep]
-            aa = T.so[:, 448 * n + Ep - 1:448 * n + 32 * Ep:Ep]
-            op("dve", lambda so=so, pat=pat, Ep=Ep, Q=Q: Vq.tensor_tensor_scan(so, T["rs%d" % pat][:, 0:32 * Ep], T[Q][:, 0:32 * Ep], 0.0, A.max, A.min),
-               dve(32 * Ep), [("rs", pat)], [Q, ("so", n)], pr)
-            j = (t + 1) % 4
-            p2 = T.m1[32 * j:32 * j + 32, 0:128]
-            gt = T.go[32 * j:32 * j + 32, 128 * n:128 * n + 128]
-            if t < RO - 1:
-                un = T.u[:, 32 * n:32 * n + 32]
-                pd = T.m1[32 * j:32 * j + 32, 128:256]
-                op("act", lambda un=un, aa=aa: Cq.activation(un, aa, F.Relu, bias=-38912.0, scale=19.0), act(32), [("so", n)], [("u", n)], pr)
-                mm([(pd, aa, T.ident[:], True, False, 32, 128), (pd, T.selt[0:32 * j, 576:608], H[ph][0:32 * j, :], False, False, 32, 128),
-                    (pd, un, T.nid[:], False, True, 32, 128),
-                    (p2, aa, T.ident[:], True, False, 32, 128), (p2, un, T.nid[:], False, True, 32, 128)],
-                   [("so", n), ("u", n), "ident", "nid", "m1"] + hkeys(ph, j - 1), [], pr)
-                op("act", lambda pd=pd, ph=ph, j=j: Cq.activation(H[ph][32 * j:32 * j + 32, :], pd, F.Relu), act(128), [], ["m1", ("h", ph, j)], pr)
-            else:
-                mm([(p2, aa, T.ident[:], True, True, 32, 128)], [("so", n), "ident", "m1"], [], pr)
-            op("act", lambda gt=gt, p2=p2: Cq.activation(gt, p2, F.Abs), act(128), [], ["m1", ("go", n)], pr + 0.022)
-            op("sync", lambda gt=gt, t=t, ph=ph: Yq.dma_start(T.yp[8 + t::16, V * ph:V * ph + V], gt), 60, [("go", n), "yp0"], [("yp", n)], pr + 0.03,
-               2000, ("outs", 16 * 2 * RO, True))
-            if t < RO - 1:
-                if ph == 0:
-                    a = 512 * (j - 1) + 128 * rank
-                    send(j, T.h0[:], T.hl[:, a:a + 128], [("h", 0, x) for x in range(4)], pr, PAR["lat"])
-                build_block(j, wblock(j, ph), T.sc[:, V * ph:V * ph + V], H[ph][0:32 * j + 32, :],
-                            [("h", ph, x) for x in range(j + 1)] + [("sc", ph)], ("w", j, ph), "m3", pr + 0.01, "act")
-                build_top(j, ph, "m2", pr + PAR["toppr"])
-                if ph == 0:
-                    for x, q in enumerate(others):
-                        a = 512 * (j - 1) + 128 * q
-                        build_block(j, W[j][:, OB + V * q:OB + V * q + V], T.scl[:, V * q:V * q + V], T.hl[0:32 * j + 32, a:a + 128],
-                                    [("arr", j), ("arr", 4)], ("wq", j, x), ("m3", "m2", "m1")[x], pr + 0.025, PAR["rem"][x])
+            for i, s in enumerate(order):
+                pr = n + i / 10.0 - (.6 if t == 0 and ph == 0 and i < 2 else 0)
+                mi = cnt["m"] % NM
+                cnt["m"] += 1
+                if s == "cp":
+                    win, off, rk = W[t][:], T.lo[:, 64 + 32 * ph:96 + 32 * ph], wkeys(t, True) + ["lo"]
+                elif s == "ys":
+                    win, off, rk = W[t][:], T.lo[:, 160:192], wkeys(t, True) + ["lo"]
+                else:
+                    win, off, rk = W[t][:, EW:WW], T.eo[:, ph, 32 * s:32 * s + 32], wkeys(t, False) + [("eo", s, ph)]
+                tt(T.m[:, V * mi:V * mi + V], win.indirect(off), T.top[:, V * ph:V * ph + V], A.max, V,
+                   rk + [("top", ph)] + [("top", n, r) for r in range(15)], [("m", mi)], pr, GA)
+                grp = []
+                for c in range(4):
+                    o = T[Q][:, 2 * c:2 * c + 2, i:8 * E:E]
+                    if s == "ys":
+                        grp.append((o, T.ident[:], T.pen[:, 4 * t + c, :], True, False, 16, 16))
+                    grp.append((o, T.m[:, V * mi + 128 * c:V * mi + 128 * c + 128], T.sp[:, 16 * t:16 * t + 16], s != "ys", True, 128, 16))
+                mm(grp, [("m", mi), ("sp", t, 0), ("sp", t, 1), Q] + ([("pen", t), "ident"] if s == "ys" else []), [], pr, 4)
+            pr = n + .9
+            hb, rr, a0 = T.hb[:, 256 * ph:256 * ph + 32 * E], T.rr[:, 256 * ph:256 * ph + 32 * E], 128 * ph + 32 * t
+            aa, un = T.aa[:, a0:a0 + 32], T.u[:, a0:a0 + 32]
+            ts(hb, T[Q][:, 1::2, 0:8 * E], MAGIC, MAGIC, A.add, A.subtract, 32 * E, [], [Q, ("topw", ph), ("hb", ph)], pr)
+            tt(rr, T[Q][:, 0::2, 0:8 * E], hb, A.subtract, 32 * E, [("hb", ph)], [Q, ("rr", ph)], pr)
+            scan(T.so[:, 256 * n:256 * n + 32 * E], T["rs%d" % E][:, 0:32 * E], rr, A.max, A.min, 16 * E, [("rs", E), ("rr", ph)], [("so", n)], pr)
+            tt(aa, T.so[:, 256 * n + E - 1:256 * n + 32 * E:E], T.a1[:, 32 * n:32 * n + 32] if t else sr, A.min, 64,
+               [("so", n), ("a1" if t else "sr", n)], [("aa", n)], pr)
+            j = t + 1
+            if t == RO - 1:
+                leave(t, ph, pr)
+                continue
+            ac(un, aa, F.Relu, 32, [("aa", n)], [("u", n)], pr, bias=-2047.0 * (8 if t else 4608), scale=8.0 if t else 4608.0)
+            b = bank("*")
+            pd = cols(b, 0, 128, 32 * j, 32 * j + 32)
+            mm([(pd, T.sel[0:kk, SN:SW], H[ph][0:kk, :], True, False, 32, 128), (pd, aa, T.ident[:], False, False, 32, 128),
+                (pd, un, T.nid[:], False, True, 32, 128)], [("aa", n), ("u", n), "ident", "nid", b] + hk(ph, t), [], pr)
+            ac(H[ph][32 * j:32 * j + 32, :], pd, F.Relu, 128, [], [b, ("h", ph, j)], pr, bias=1.0)
+            if ph == 0:
+                a = 512 * t + 128 * rank
+                send(j, T.h0[:], T.hl[:, a:a + 128], [("h", 0, x) for x in range(4)], pr, PAR["lat"])
+            build(j, [wblock(j, ph)], T.pq[:, V * ph:V * ph + V], H[ph][0:32 * j + 32, :], [("h", ph, x) for x in range(j + 1)] + pqk[ph],
+                  [("w", j, ph)], pr + .01, dict(a="act", d="dve")[PAR["wown"][n]])
+            c0, rows = (own0, 0)[ph], list(range(8)) + GAINED[j]
+            for r in rows:
+                op("sync", lambda r=r, j=j, ph=ph, c0=c0: Yq.dma_start(T.top[r::16, V * ph:V * ph + V], W[j][15::16, c0:c0 + V]), PAR["dq"],
+                   [("w", j, ph), ("topw", ph)], [("top", 2 * j + ph, r)], pr, PAR["dlat"], ("tp%d" % (2 * j + ph), 16 * len(rows), True))
+            kept(j, ph, pr + .5)
     return ops
 
 
-def schedule(ops):
-    n = len(ops)
-    users = [[] for _ in range(n)]
-    left = [len(o["deps"]) for o in ops]
-    for i, o in enumerate(ops):
-        for d in o["deps"]:
-            users[d].append(i)
-    ready = [0.0] * n
-    avail = {}
+def place(case, before, seq, back):
+    hop = PAR["hop"]
+    busy = dict(dve=[], act=[], pe=[], pool=[], sync=[])
+    end = [0.0] * len(seq)
+    for i in seq:
+        e, _, cost, lat = case[i]
+        if back:
+            t0 = max([end[d] for d in before[i]] + [0.0]) + lat + hop
+        else:
+            t0 = max([end[d] + case[d][3] + hop for d in before[i]] + [0.0])
+        lst = busy[e]
+        x = len(lst)
+        while x and lst[x - 1][1] > t0:
+            x -= 1
+        while x < len(lst) and lst[x][0] < t0 + cost:
+            t0 = max(t0, lst[x][1])
+            x += 1
+        lst.insert(x, (t0, t0 + cost))
+        end[i] = t0 + cost
+    return end
+
+
+def schedule(case, users, key, rnd, noise):
+    n = len(case)
+    deps = [c[1] for c in case]
+    key = [x + noise * rnd() for x in key]
     for i in range(n):
-        if left[i] == 0:
-            avail.setdefault(ops[i]["eng"], []).append(i)
-    free = {}
-    order = []
-    while len(order) < n:
-        best = None
-        for e, lst in avail.items():
-            if not lst:
-                continue
-            t0 = max(free.get(e, 0.0), min(ready[i] for i in lst))
-            i = min((i for i in lst if ready[i] <= t0 + PAR["look"]), key=lambda i: (ops[i]["prio"], i))
-            t0 = max(t0, ready[i])
-            if best is None or t0 < best[0]:
-                best = (t0, i, e)
-        t0, i, e = best
-        avail[e].remove(i)
-        free[e] = t0 + ops[i]["cost"]
-        order.append(i)
-        for u in users[i]:
-            ready[u] = max(ready[u], free[e] + ops[i]["lat"] + PAR["hop"])
-            left[u] -= 1
-            if left[u] == 0:
-                avail.setdefault(ops[u]["eng"], []).append(u)
-    return order
+        for d in deps[i]:
+            key[i] = max(key[i], key[d] + 1e-3)
+    seq = sorted(range(n), key=lambda i: key[i])
+    for _ in range(2):
+        end = place(case, deps, seq, False)
+        end = place(case, users, sorted(range(n), key=lambda i: -end[i]), True)
+        seq = sorted(range(n), key=lambda i: -end[i])
+    end = place(case, deps, seq, False)
+    return max(end), [end[i] - case[i][2] for i in range(n)]
 
 
 def span(case, order):
@@ -444,79 +588,184 @@ def span(case, order):
     done = [0.0] * len(order)
     for i in order:
         e, deps, cost, lat = case[i]
-        t0 = free[e]
-        for d in deps:
-            if done[d] > t0:
-                t0 = done[d]
+        t0 = max([free[e]] + [done[d] for d in deps])
         free[e] = t0 + cost
         done[i] = t0 + cost + lat + hop
     return max(done)
 
 
-def choose(g, core, T, topo, rank):
-    if "order" in KEPT:
-        return plan(g, core, T, topo, rank), KEPT["order"]
-    base = dict(PAR)
-    cases = []
-    for c in CASES:
-        PAR.update(c)
-        cases.append([(o["eng"], tuple(o["deps"]), o["cost"], o["lat"]) for o in plan(g, core, T, topo, rank)])
-    seed = [12345]
+def anneal(case, start0, marks, rnd, moves, hot):
+    names = ["dve", "act", "pe", "pool", "sync"]
+    eng = [names.index(c[0]) for c in case]
+    deps = [list(c[1]) for c in case]
+    cost = [c[2] for c in case]
+    lat = [c[3] + PAR["hop"] for c in case]
+    n, amp = len(case), PAR["amp"]
 
-    def rnd():
-        seed[0] = (seed[0] * 1103515245 + 12345) % 2147483648
-        return seed[0] / 2147483648.0
+    def decode(seq, p0, p1, start, done, S, Z):
+        dirty = -1.0
+        for p in range(p0, n):
+            i = seq[p]
+            old = start[i]
+            if p >= p1 and old > dirty:
+                return p
+            t0 = 0.0
+            for d in deps[i]:
+                if done[d] > t0:
+                    t0 = done[d]
+            s, z, c = S[eng[i]], Z[eng[i]], cost[i]
+            if not z or z[-1] <= t0:
+                s.append(t0)
+                z.append(t0 + c)
+            else:
+                m = x = len(z)
+                while x and z[x - 1] > t0:
+                    x -= 1
+                while x < m and s[x] < t0 + c:
+                    t0 = z[x]
+                    x += 1
+                s.insert(x, t0)
+                z.insert(x, t0 + c)
+            if t0 != old:
+                old = (t0 if t0 > old else old) + c + lat[i] + 1.0
+                if old > dirty:
+                    dirty = old
+                start[i] = t0
+                done[i] = t0 + c + lat[i]
+        return n
 
-    def value(order):
-        val = 1.0
-        for c in cases:
-            val *= span(c, order) / 1e5
-        return val
+    def value(done):
+        v = max(done)
+        for i, w in marks:
+            v += w * done[i]
+        return v
 
-    best = None
-    for k in range(base["tries"]):
-        PAR.update(ga=1.25 + .65 * rnd(), ao=60 + 80 * rnd(), pc=.42 + .3 * rnd(), lat=2800 + 1500 * rnd(), look=40 + 200 * rnd())
-        ops = plan(g, core, T, topo, rank)
-        order = schedule(ops)
-        val = value(order)
-        if best is None or val < best[0]:
-            best = (val, ops, order)
-    PAR.update(base)
-    val, ops, order = best
-    n = len(order)
-    for k in range(base["moves"]):
-        a = int(rnd() * n)
-        e = ops[order[a]]["eng"]
-        b = a + 1
-        skip = int(rnd() * 2.5)
-        while b < n and (ops[order[b]]["eng"] != e or skip):
-            skip -= ops[order[b]]["eng"] == e
-            b += 1
-        if b >= n:
-            continue
-        seg = order[a:b + 1]
+    def counts(seq):
+        c, out = [0] * 5, []
+        for i in seq:
+            out.append(tuple(c))
+            c[eng[i]] += 1
+        return out + [tuple(c)]
+
+    seq = sorted(range(n), key=lambda i: start0[i])
+    start, done = [-1.0] * n, [0.0] * n
+    S, Z = [[] for _ in names], [[] for _ in names]
+    decode(seq, 0, n, start, done, S, Z)
+    val = value(done)
+    seq.sort(key=lambda i: start[i])
+    pre = counts(seq)
+    best = (val, seq, start)
+    for it in range(moves):
+        p = int(rnd() * n)
+        i, step = seq[p], amp * rnd() ** 2
         if rnd() < 0.5:
-            take = {seg[-1]}
-            for i in reversed(seg[:-1]):
-                if any(i in ops[u]["deps"] for u in take):
-                    take.add(i)
-            if seg[0] in take:
+            lim, b = start[i] + step, p + 1
+            while b < n and start[seq[b]] < lim:
+                b += 1
+            take, front, back = {i}, [], [i]
+            for j in seq[p + 1:b]:
+                for d in deps[j]:
+                    if d in take:
+                        take.add(j)
+                        back.append(j)
+                        break
+                else:
+                    front.append(j)
+            if not front:
                 continue
-            new = [i for i in seg if i in take] + [i for i in seg if i not in take]
+            new, p0, p1 = seq[:p] + front + back + seq[b:], p, b
         else:
-            take = {seg[0]}
-            for i in seg[1:]:
-                if ops[i]["deps"] & take:
-                    take.add(i)
-            if seg[-1] in take:
+            lim, a = start[i] - step, p
+            while a > 0 and start[seq[a - 1]] > lim:
+                a -= 1
+            need, front, back = set(deps[i]), [i], []
+            for j in reversed(seq[a:p]):
+                if j in need:
+                    need.update(deps[j])
+                    front.append(j)
+                else:
+                    back.append(j)
+            if not back:
                 continue
-            new = [i for i in seg if i not in take] + [i for i in seg if i in take]
-        cand = order[:a] + new + order[b + 1:]
-        v = value(cand)
-        if v <= val:
-            val, order = v, cand
-    KEPT["order"] = order
-    return ops, order
+            new, p0, p1 = seq[:a] + front[::-1] + back[::-1] + seq[p + 1:], a, p + 1
+        left = pre[p0]
+        S2, Z2 = [S[e][:left[e]] for e in range(5)], [Z[e][:left[e]] for e in range(5)]
+        st2, dn2 = list(start), list(done)
+        p = decode(new, p0, p1, st2, dn2, S2, Z2)
+        v = value(dn2)
+        if v <= val or rnd() < math.exp((val - v) / (hot * (PAR["cold"] / hot) ** (it / moves))):
+            left = pre[p]
+            val, start, done = v, st2, dn2
+            S, Z = [S2[e] + S[e][left[e]:] for e in range(5)], [Z2[e] + Z[e][left[e]:] for e in range(5)]
+            seq = sorted(new, key=lambda i: st2[i])
+            pre = counts(seq)
+            if v < best[0]:
+                best = (v, seq, start)
+    return best[1], list(best[2]), best[0]
+
+
+def choose(g, core, T, topo, rank):
+    if "order" not in KEPT:
+        seed = [12345]
+
+        def rnd():
+            seed[0] = (seed[0] * 1103515245 + 12345) % 2147483648
+            return seed[0] / 2147483648.0
+
+        ops = plan(g, core, T, topo, rank)
+        n = len(ops)
+        free = [(o["eng"], tuple(o["deps"] | o["soft"]), o["cost"], o["lat"]) for o in ops]
+        users = [[] for _ in ops]
+        first, last = {}, {}
+        for i, o in enumerate(ops):
+            for d in free[i][1]:
+                users[d].append(i)
+            for b in o["r"] + o["w"]:
+                if b in KEPT["kind"]:
+                    (first if o["eng"] == "pe" else last).setdefault(b, []).append(i)
+        marks = [(i, PAR["marks"][o["w"][-1][0]]) for i, o in enumerate(ops)
+                 if o["w"] and o["w"][-1] not in KEPT["kind"] and o["w"][-1][0] in PAR["marks"]]
+
+        def banks(start):
+            bank, more, held = {}, {}, {}
+            for b in sorted(first, key=lambda b: min(start[i] for i in first[b])):
+                names = dict(g=GB, d=DB)[KEPT["kind"][b]] if KEPT["kind"][b] != "*" else GB + DB
+                t0 = min(start[i] for i in first[b])
+                x = min(names, key=lambda x: (max(held.get(x, (0, 0))[0], t0 - 300), rnd()))
+                for i in first[b]:
+                    more[i] = tuple(last[held[x][1]]) if x in held else ()
+                bank[b], held[x] = x, (max(start[i] + free[i][2] for i in last[b]), b)
+            case = [(c[0], c[1] + more.get(i, ()), c[2], c[3]) for i, c in enumerate(free)]
+            moved = True
+            while moved:
+                moved = False
+                for i in range(n):
+                    for d in case[i][1]:
+                        if start[i] <= start[d]:
+                            start[i], moved = start[d] + 1e-3, True
+            return bank, more, case
+
+        def improve(start, steps, keep):
+            for moves, hot, weight in steps:
+                bank, more, case = banks(start)
+                order, start, val = anneal(case, start, [(i, w * weight) for i, w in marks], rnd, moves, hot)
+                val = span(case, order)
+                if keep is None or val < keep[0]:
+                    keep = (val, order, bank, more, case, list(start))
+            return keep
+
+        keep = None
+        for s in range(PAR["starts"]):
+            best = (1e18, [max(o["prio"], -3) * 8000 + o["prio"] for o in ops])
+            for k in range(PAR["tries"]):
+                best = min(best, schedule(free, users, best[1], rnd, PAR["noise"] * rnd()))
+            keep = improve(anneal(free, best[1], marks, rnd, PAR["first"], 200.0)[1], PAR["steps"], keep)
+        keep = improve(list(keep[5]), PAR["more"], keep)
+        KEPT.update(order=keep[1], bank=keep[2], more=keep[3], cases=[keep[4]])
+    ops = plan(g, core, T, topo, rank)
+    for i, d in KEPT["more"].items():
+        ops[i]["deps"] |= set(d)
+    return ops, KEPT["order"]
 
 
 def rank_program(g, core, T, topo):
@@ -551,7 +800,7 @@ def rank_program(g, core, T, topo):
             count[e] = count.get(e, 0) + 1
             ins.then_inc(S[e], 1)
             token[i] = (e, count[e])
-    g.sync.wait_ge(S.outs, 16 * 2 * RO)
+    g.sync.wait_ge(S.outs, 16 * 8 * RO)
     for o in ops:
         if o["sem"] is not None and not o["sem"][2]:
             g.wait_ge(S[o["sem"][3]], o["sem"][4])

import math
from concourse.bass import DstId, RemoteDMATransfer
from concourse.mybir import AluOpType as A, ActivationFunctionType as F

NR, V, RO = 4, 512, 4
OB, EW, WW = 520, 512, 2568
K, KD, MAGIC = 4096, 4096.0, 1.5 * 2.0 ** 35
NPS, NX, L = (5, 6), 6, 11
XW = 8 * NX * L
NM = 12
SN, SW = 512, 544
XL = [9, 9, 10, 11]
XO = [0, 0, 32 * NX * 9, 32 * NX * 19, 32 * NX * 30]
GW = 32 * NX
GAINED = [[], [9, 10, 13], [9, 10, 11, 14], [9, 10, 11, 12, 13]]


def _sb(n, dt):
    return ("sbuf", [128, n], dt)


H16, B16, F32 = "float16", "bfloat16", "float32"
SCRATCH = {
    "pi": _sb(1024, "int32"), "x16": _sb(1024, H16), "u16": _sb(1024, H16), "pq": _sb(1024, H16), "land": _sb(2048, H16),
    "li": _sb(192, "int32"), "lt": _sb(192, F32), "lu": _sb(192, F32), "lo": _sb(192, "uint16"), "eo": ("sbuf", [128, 2, 352], "uint16"),
    "hl": _sb(3 * 512, H16), "out0": _sb(1024, F32), "w0": _sb(WW, F32), "w1": _sb(WW, F32), "w2": _sb(WW, F32), "w3": _sb(WW, F32),
    "m": _sb(NM * 512, F32), "top": _sb(2 * 512, F32), "xl": _sb(4 * 1024, H16), "xx": _sb(4 * 512, H16), "ab": _sb(256, F32),
    "zx": _sb(352, H16), "pen": ("sbuf", [128, 16, 16], H16), "so": _sb(8 * 256, H16), "sr": _sb(8 * GW, H16), "aa": _sb(256, H16), "u": _sb(256, H16),
    "hb": _sb(512, F32), "rr": _sb(512, H16), "h0": _sb(128, H16), "h1": _sb(128, H16), "go": _sb(256, F32), "t0": _sb(512, H16),
    "raw0": _sb(NX * 512, H16), "raw1": _sb(NX * 512, H16), "xt0": _sb(XO[RO], H16), "xt1": _sb(XO[RO], H16),
    "xm0": ("sbuf", [128, GW, L], H16), "xm1": ("sbuf", [128, GW, L], H16), "seld": ("sbuf", [128, 32, NX * L], B16),
    "ro0": _sb(4 * XW, H16), "ro1": _sb(4 * XW, H16), "pick9": _sb(72, B16), "db": _sb(1024, B16), "r0": _sb(256, B16), "e16": _sb(8, H16),
    "gt": _sb(8 * GW, H16), "zb": _sb(2 * GW, F32), "zs": _sb(8 * GW, H16), "a1": _sb(256, H16),
    "zero": _sb(XW, B16), "ident": _sb(128, B16), "nid": _sb(128, B16), "nkd": _sb(128, B16),
    "dx": _sb(128, B16), "du": _sb(128, B16), "ws0": _sb(128, B16), "ws1": _sb(128, B16), "pick": _sb(64, B16),
    "sel": _sb(SW, B16), "selw": _sb(512, B16), "am": _sb(8 * 144, B16), "ownf": _sb(8, F32), "own": _sb(256, B16),
    "tab": _sb(256, F32), "mi": _sb(256, "int32"), "mj": _sb(256, "int32"), "mk": _sb(256, F32), "tm": _sb(256, F32), "tz": _sb(256, F32),
    "ts": _sb(256, F32), "one": _sb(8, F32), "dg0": _sb(8, F32), "dg": _sb(8, F32), "sp": _sb(64, F32),
}
for _e in range(3, 9):
    SCRATCH["rs%d" % _e] = _sb(256, B16)
GB, DB = ["g0", "g1", "g2"], ["d0", "d1", "d2"]
for _b in DB:
    SCRATCH[_b] = ("psum", [128, 512], F32)
for _b in GB + ["q0", "q1"]:
    SCRATCH[_b] = ("psum", [128, 8, 64], F32)
SEMAPHORES = ["dve", "act", "pe", "pool", "ldo", "ldp", "ldt", "ldl", "rep", "o0", "outs", "ar0", "ar1", "ar2", "ar3",
              "sent0", "sent1", "sent2", "sent3", "tp2", "tp3", "tp4", "tp5", "tp6", "tp7"]

PAR = dict(cy=.85, ga=1.56, pc=.43, po=0.0, hop=100.0, ao=70.0, vo=55.0, lat0=4200.0, lat=3000.0, dq=100.0, dlat=2300.0,
           tries=40, starts=4, first=10000, steps=((20000, 200.0, 1.0), (20000, 80.0, 1.0)),
           more=((80000, 100.0, 1.0), (80000, 50.0, .4), (60000, 30.0, .15)), marks=dict(arr=1.0, aa=0.3, wq=0.2),
           cold=10.0, amp=4000.0, noise=3000.0, rem=(("act",) * 3,) * 3, x0=("act", "dve", "act", "dve"),
           ob=(0, 0, 0, 0, 0, 0, 4, 3), wown="daaaaa", lde="aadadaaa", xse="aaaa", rd=[[4]] + [[]] * 7,
           rg=([[0], [1], [2], [3], [4]], [[0, 1], [2, 3], [4, 5]]))
KEPT = {}


def dve(n, f=1.0):
    return PAR["vo"] + max(64, n * f) * PAR["cy"]


def act(n, f=1.0):
    return PAR["ao"] + max(64, n * f) * PAR["cy"]


def pool(n):
    return 170 + 2 * n * PAR["cy"]


def table():
    t = [[0.0] * 16 for _ in range(16)]
    for r in range(RO):
        for p in list(range(8)) + GAINED[r]:
            t[r][p] = t[4 + r][p] = 1.0 - 2 * (p % 2)
        t[r][8], t[4 + r][8] = (0.625 if r else 0.5), 0.3125
    t[8], t[9] = [float(K)] * 16, [-1025.0 * K] * 16
    t[8][8], t[9][8] = 0.0, 4096.0
    t[10] = [0.0] * 8 + [1.0] * 8
    t[11][8] = 1.0
    for c in (12, 13):
        t[c][:8] = [-1024.0 * K, -1025.0 * K] * 3 + [-1024.0 * K, 2048 - 1025.0 * K]
    t[13][8:] = [-1.0, -1025.0 * K - 2049, -1025.0 * K, -1026.0 * K, -1025.0 * K, -1026.0 * K + 2561, -1025.0 * K - 2561, -1025.0 * K]
    t[14] = [1.0] * 16
    t[14][9] = t[14][14] = K + 1.0
    t[14][13], t[14][15] = K - 1.0, float(K)
    t[15] = [2048.0] * 8 + [2048.0 - K] * 8
    return [x for c in t for x in c]


def paints():
    want = table()
    base = [(0, 128, 2, 1.0), (1, 128, 2, -1.0), (128, 256, 1, 0.0)]
    have = [1.0, -1.0] * 64 + [0.0] * 128
    rest, used = [], set()
    for val in sorted(set(want)):
        need = set(i for i in range(256) if want[i] == val and have[i] != val)
        while need:
            best = None
            for a in sorted(need):
                for st in range(1, 130):
                    n, hit = 0, 0
                    while a + n * st < 256 and want[a + n * st] == val and a + n * st not in used:
                        hit += a + n * st in need
                        n += 1
                    if best is None or hit > best[0]:
                        best = (hit, a, st, n)
            _, a, st, n = best
            rest.append((a, a + (n - 1) * st + 1, st, val))
            need -= set(range(a, a + n * st, st))
            used |= set(range(a, a + n * st, st))
    return base, rest


def plan(g, core, T, topo, rank):
    S = T.sem
    GA = PAR["ga"]
    Vq, Cq, Pq, Yq = g.vector, g.scalar, g.tensor, g.sync
    ops, last_w, readers = [], {}, {}

    def op(eng, fn, cost, r=(), w=(), prio=0.0, lat=0.0, sem=None, soft=()):
        i = len(ops)
        deps, war = set(), set()
        for k in r:
            if k in last_w:
                deps.add(last_w[k])
        for k in w:
            if k in last_w:
                deps.add(last_w[k])
            war.update(readers.get(k, ()))
        for k in r:
            readers.setdefault(k, []).append(i)
        for k in w:
            last_w[k] = i
            readers[k] = []
        war -= deps
        deps |= war
        deps.discard(i)
        ops.append(dict(eng=eng, fn=fn, cost=cost, deps=deps, war=war, prio=prio, lat=lat, sem=sem, r=list(r), w=list(w),
                        soft=set(last_w[k] for k in soft if k in last_w)))
        return i

    def mm(group, r, w, prio, f=1):
        def fn():
            ins = None
            for (o, l, rh, st, sp, _m, _n) in group:
                ins = Pq.matmul(o, l, rh, st, sp)
            return ins
        return op("pe", fn, sum(PAR["po"] + f * max(min(64, x[5]), x[6]) * PAR["pc"] for x in group), r, w, prio)

    def ac(out, in_, func, n, r, w, prio, f=1.0, **kw):
        op("act", lambda: Cq.activation(out, in_, func, **kw), act(n, f), r, w, prio)

    def ts(out, in_, a, b, o0, o1, n, r, w, prio, f=1.0):
        if o1 is None:
            op("dve", lambda: Vq.tensor_scalar(out, in_, a, None, o0), dve(n, f), r, w, prio)
        else:
            op("dve", lambda: Vq.tensor_scalar(out, in_, a, b, o0, o1), dve(n, f), r, w, prio)

    def ev(eng, out, in_, n, r, w, prio, scale=1.0, bias=0.0):
        if eng == "act":
            ac(out, in_, F.Identity, n, r, w, prio, scale=scale, bias=bias)
        else:
            ts(out, in_, scale, bias, A.mult, A.add, n, r, w, prio)

    def fill(out, val, n, w, prio, r=()):
        op("dve", lambda: Vq.memset(out, val), dve(n), r, w, prio)

    def tt(out, a, b, alu, n, r, w, prio, f=1.0):
        op("dve", lambda: Vq.tensor_tensor(out, a, b, alu), dve(n, f), r, w, prio)

    def scan(out, a, b, o0, o1, n, r, w, prio):
        op("dve", lambda: Vq.tensor_tensor_scan(out, a, b, 0.0, o0, o1), dve(n), r, w, prio)

    def sel(out, in_, pattern, val, base, r, w, prio, n, cm=-1):
        op("pool", lambda: g.affine_select(out, in_, pattern, A.not_equal, val, base, cm), pool(n), list(r) + ["ps"], w, prio)

    def iota(out, pattern, base, cm, w, prio, n):
        op("pool", lambda: g.iota(out, pattern, base, cm, allow_small_or_imprecise_dtypes=True), pool(n), ["ps"], w, prio)

    cnt = dict(m=0, g=0)
    kinds = KEPT.setdefault("kind", {})

    def bank(kind="g"):
        cnt["g"] += 1
        kinds[cnt["g"]] = kind
        return cnt["g"]

    def B(b):
        return T[KEPT.get("bank", {}).get(b, "d0" if kinds[b] == "d" else "g0")]

    def cols(b, a, n, p0=0, p1=128):
        t = B(b)
        if len(t.shape) == 2:
            return t[p0:p1, a:a + n]
        return t[p0:p1, a // 64:(a + n) // 64, :] if n >= 64 else t[p0:p1, a // 64, a % 64:a % 64 + n]

    W = [T.w0, T.w1, T.w2, T.w3]
    H, RAW, XT, RS, XM = [T.h0, T.h1], [T.raw0, T.raw1], [T.xt0, T.xt1], [T.ro0, T.ro1], [T.xm0, T.xm1]
    others = [q for q in range(NR) if q != rank]
    peers = [T.cores[q] for q in others]
    mask = -1
    for c in peers:
        mask &= topo.mask(core, c)
    dsts = [DstId(rid=topo.addr(c)[0], pnc=topo.addr(c)[1]) for c in peers]
    own0 = OB + V * rank

    def col(c):
        return T.ts[:, 16 * c + 15:16 * c + 16]

    def wblock(t, ph):
        return W[t][:, own0:own0 + V] if ph == 0 else W[t][:, 0:V]

    def send(k, src, dst, r, prio, lat):
        def fn():
            g.remote_dma_fused([RemoteDMATransfer(dst_ids=dsts, dma_engine_mask=mask, remote_sem=S["ar%d" % k],
                                                  srcs=[src], dsts=[dst] * len(dsts))], local_sem=S["sent%d" % k])
            return None
        ne = bin(mask).count("1")
        op("pool", fn, 500, r, [("arr", k)], prio, lat, sem=("ar%d" % k, ne * len(dsts), False, "sent%d" % k, ne))

    op("sync", lambda: Yq.dma_start(T.pi[:, 0:256], T.pts[:, 0:256]), 60, [], [("pi", 0)], -300, 2300, ("ldo", 16, True))
    op("act", lambda: Cq.dma_start(T.pi[:, 256:V], T.pts[:, 256:V]), 60, [], [("pi", 1)], -500, 2500, ("ldp", 16, True))
    for j, (nm, a, b) in enumerate([("ld", 0, 64), ("cp", 64, 128), ("xs", 128, 160), ("ys", 160, 192)]):
        op("sync", lambda nm=nm, a=a, b=b: Yq.dma_start(T.li[:, a:b], T[nm][:]), 60, [], [("li", j)], -298 + j, 3000, ("ldl", 64, True), [("pi", 0)])
    op("sync", lambda: Yq.dma_start(T.pi[:, V:], T.pts[:, V:]), 60, [], [("pi", 2), ("pi", 3)], -290, 1400, ("ldt", 16, True), [("pi", 0)])

    Z = T.zero
    fill(Z[:], 0.0, XW // 2, ["zero"], -400)
    sel(T.dx[:], Z[:, 0:128], [[16, 8], [0, 2], [1, 8]], 1.0, 0, ["zero"], ["dx"], -399, 128)
    sel(T.du[:], Z[:, 0:128], [[16, 8], [-1000, 2], [1, 8]], -K / 512.0, 1000, ["zero"], ["du"], -398, 128)
    op("pool", lambda: g.iota(T.mi[:], [[0, 16], [1, 16]], 128, -1), pool(256), ["ps"], ["mi"], -401)
    ts(T.mj[:], T.mi[:], 15, None, A.bitwise_and, None, 256, ["mi"], ["mj"], -397)
    ts(T.mk[:], T.mj[:], 0.0, None, A.is_equal, None, 256, ["mj"], ["mk"], -396)
    if "paints" not in KEPT:
        KEPT["paints"] = paints()
    base, rest = KEPT["paints"]
    for j, (a, b, st, val) in enumerate(base):
        fill(T.tab[:, a:b:st], val, 64, [("tb", j)], -399)
    for j, (a, b, st, val) in enumerate(rest):
        n = len(range(a, b, st))
        if j % 2:
            fill(T.tab[:, a:b:st], val, n, [("tr", j)], -398, [("tb", x) for x in range(3)])
        else:
            ac(T.tab[:, a:b:st], Z[:, 0:n], F.Identity, n, ["zero"] + [("tb", x) for x in range(3)], [("tr", j)], -398, bias=val)
    fill(T.tz[:], 1.0, 256, ["tz"], -395)
    fill(T.tz[:, 0::16], 0.0, 16, ["tz"], -395)
    tt(T.tm[:], T.tab[:], T.mk[:], A.mult, 256, ["mk"] + [("tr", j) for j in range(len(rest))], ["tm"], -394, 2)
    scan(T.ts[:], T.tz[:], T.tm[:], A.mult, A.add, 256, ["tz", "tm"], ["col"], -393)
    for par in range(2):
        sg = 1.0 - 2 * par
        sel(T.ws1[:, par::2], Z[:, 0:64], [[16, 8], [1000, 2], [2, 4]], -sg, 1 + par, ["zero"], [("ws", par)], -390, 64)
        if par:
            sel(T.ws1[:, 7::16], T.ws1[:, 7::16], [[16, 8]], 0.0, 8, [], [("ws", par)], -389, 8)
        sel(T.ws1[:, par::2], T.ws1[:, par::2], [[16, 8], [1000, 2], [2, 4]], sg, 8 + par, [], [("ws", par)], -388, 64)
    sel(T.ws1[:], T.ws1[:], [[16, 8], [1000, 2], [1, 8]], float(K), 0, [], [("ws", 0), ("ws", 1), "ws1"], -387, 128)
    sel(T.ws0[:], T.ws1[:], [[16, 8], [-1000, 2], [1, 8]], 1.0, 1008, ["ws1"], ["ws0"], -386, 128)
    sel(T.pick[:], Z[:, 0:64], [[16, 8], [-1, 8]], 1.0, 15, ["zero"], ["pick"], -385, 64)
    iota(T.r0[:], [[0, 32], [4096, 8]], -1, 0, ["r0"], -384.9, 256)
    sel(T.ident[:], Z[:, 0:128], [[1, 128]], 1.0, 0, ["zero"], ["ident"], -384.8, 128)
    sel(T.sel[0:32, 0:512], Z[0:32, 0:512], [[1, 32], [0, 16]], 1.0, 0, ["zero"], ["selt"], -383, 512)
    fill(T.one[:], 1.0, 8, ["one"], -396)
    op("pool", lambda: g.affine_select(T.dg0[:], T.one[:], [[-16, 8]], A.is_ge, 0.0, 0, 1), pool(8), ["one", "ps"], ["dg0"], -384.7)
    op("pool", lambda: g.affine_select(T.dg[:], T.dg0[:], [[16, 8]], A.is_ge, 0.0, 15, -1), pool(8), ["dg0", "ps"], ["dg"], -384.6)
    for t in range(RO):
        for x in range(2):
            ev(("act", "dve")[x], T.sp[:, 16 * t + 8 * x:16 * t + 8 * x + 8], T.dg[:], 8, ["dg", "col"], [("sp", t, x)], -196 + t, col(4 * x + t))
    fill(T.pen[:, :, :], 0.0, 128, [("pen", t) for t in range(RO)], -60)
    for s in range(8):
        sel(T.am[:, 144 * s:144 * s + 144], Z[:, 0:144], [[16, 9], [1000, 16]], 1.0, 8 + s - 15000, ["zero"], [("am", s)], -190 + s, 144)
    sel(T.pick9[:], Z[:, 0:72], [[16, 8], [-1, 9]], 1.0, 16, ["zero"], ["pick9"], -182, 72)
    sel(T.pick9[:], T.pick9[:], [[16, 8], [0, 9]], -1.0, 0, [], ["pick9"], -182, 72)
    sel(T.pick9[:, 0::9], Z[:, 0:8], [[16, 8]], 2560.0, 0, [], ["pick9"], -182, 8)
    iota(T.own[:], [[-128, 4], [0, 64]], -V * rank, 0, ["own"], -180, 256)
    iota(T.ownf[:, 0:1], [[0, 1]], 0, -1, ["ownf"], -180, 1)
    for nm, val, pr in (("nid", -1.0, -175), ("nkd", -KD, -171)):
        sel(T[nm][:], Z[:, 0:128], [[1, 128]], val, 0, ["zero"], [nm], pr, 128)
    for c in range(4):
        sel(T.seld[0:32, 8 * c:8 * c + 8, :], Z[0:32, 0:XW], [[1, 8], [0, NX * L]], KD, 8 * c, ["zero"], [("seld", c)], -170 + c, XW)
    sel(T.sel[0:32, SN:SW], Z[0:32, 0:32], [[1, 32]], -1.0, 0, ["zero"], ["ni"], -160, 32)
    s0k = ["selt", "ni"] + [("seld", c) for c in range(4)]
    for j in range(1, 4):
        op("sync", lambda j=j: Yq.dma_start(T.sel[32 * j:32 * j + 32, :], T.sel[0:32, :]), 60, s0k, [("rep", j)], -50, 2500, ("rep", 96, True))
        op("sync", lambda j=j: Yq.dma_start(T.seld[32 * j:32 * j + 32, :, :], T.seld[0:32, :, :]), 60, s0k, [("rep", j + 3)], -50, 2500, ("rep", 96, True))
    rep = [("rep", j) for j in range(1, 7)]
    ac(T.selw[:], Z[:, 0:512], F.Identity, 512, ["zero"], ["selw0"], -98)
    swk = []
    for r in (8, 13, 14, 15):
        swk.append(("selw", r))
        sel(T.selw[:, r::16], T.sel[:, r:512:16], [[0, 32]], 0.0, 1000, ["selw0", "selt"] + rep, [swk[-1]], -40, 32)
    fill(T.h0[:], 0.0, 64, [("h", 0, x) for x in range(4)], -390)
    for e in sorted(set(NPS) | set(10 + t - ph - NPS[ph] for t in range(RO) for ph in range(2))):
        iota(T["rs%d" % e][:, 0:32 * e], [[0, 32], [-4096, e]], 2560, 0, [("rs", e)], -170 + 5 * e, 32 * e)
    for r, ws in ((9, [1]), (10, [K, -1]), (11, [K, K, 1]), (12, [K, K, K, -1])):
        for j, val in enumerate(ws):
            swk.append(("selw", r, j))
            sel(T.selw[32 * j:32 * j + 32, r::16], Z[32 * j:32 * j + 32, 0:32], [[1, 32]], float(val), 0, ["selw0"], [swk[-1]] + ["ps"] * (j > 0), -45 + j, 32)
    for ph in range(2):
        n = 64 * NPS[ph]
        sel(XM[ph][:, 0:n // 2, 0:2], Z[:, 0:n], [[0, n]], 2560.0, 0, ["zero"], [("xm", ph, c) for c in range(4)], -20, n, 0)

    def copy(out, in_, r, w, prio, n):
        sel(out, in_, [[0, n]], 0.0, 1000, r, w, prio, n)

    def build(j, out, st, hist, r, w, prio, eng, n=V):
        b = bank("*")
        src = cols(b, 0, n)
        grp = [(src, (T.ws1, T.ws0)[j == 0][:], st, True, hist is None, 128, n)]
        if hist is not None:
            grp += [(cols(b, 128 * c, 128), T.selw[0:32 * j + 32, 128 * c:128 * c + 128], hist, False, c == 3, 128, 128) for c in range(4)]
            r = r + swk
        mm(grp, r + ["ws0", "ws1", b], [], prio)
        for o, k in zip(out, w):
            ev(eng, o, src, n, ["col"], [b, k], prio, col(14) if j else 1.0, col(13 if j else 12))

    for ph in range(2):
        a, pr = V * ph, -350 + 100 * ph
        for c0, n in ((0, 256), (256, 256)) if ph == 0 else ((V, V),):
            ks = range(c0 // 256, (c0 + n) // 256)
            ts(T.x16[:, c0:c0 + n], T.pi[:, c0:c0 + n], 2048.0, None, A.min, None, n, [("pi", x) for x in ks], [("x16", x) for x in ks], pr)
            ac(T.u16[:, c0:c0 + n], T.pi[:, c0:c0 + n], F.Relu, n, [("pi", x) for x in ks], [("u16", x) for x in ks], pr, bias=-2048.0)
        for hf in range(2):
            c0, b = a + 256 * hf, bank("*")
            mm([(cols(b, 0, 256), T.dx[:], T.x16[:, c0:c0 + 256], True, False, 128, 256),
                (cols(b, 0, 256), T.du[:], T.u16[:, c0:c0 + 256], False, True, 128, 256)],
               [("x16", 2 * ph + hf), ("u16", 2 * ph + hf), "dx", "du", b], [], pr + 1)
            ev(("act", "dve")[hf], T.pq[:, c0:c0 + 256], cols(b, 0, 256), 256, [], [b, ("pq", ph, hf)], pr + 2)
        if ph == 0:
            send(0, T.pq[:, 0:V], T.land[:, V * rank:V * rank + V], [("pq", 0, 0), ("pq", 0, 1)], -500, PAR["lat0"])
    pqk = [[("pq", ph, 0), ("pq", ph, 1)] for ph in range(2)]
    ts(T.lt[:], T.li[:], 2048.0, -2568.0, A.is_ge, A.mult, 192, [("li", j) for j in range(4)], ["lt"], -145)
    tt(T.lu[:], T.lt[:], T.li[:], A.add, 192, ["lt"], ["lu"], -144, 2)
    ts(T.lo[:], T.lu[:], float(OB), None, A.add, None, 192, ["lu"], ["lo"], -143)

    def hk(ph, j):
        return [("h", ph, x) for x in range(j + 1)] + s0k[:2] + (rep if j else [])

    for ph in range(2):
        pr = -240 + 10 * ph
        build(0, [wblock(0, ph)], T.pq[:, V * ph:V * ph + V], None, pqk[ph], [("w", 0, ph)], pr + 3, ("dve", "act")[ph])
        b, b2, b3 = bank("d"), bank("*"), bank("*")
        mm([(B(b)[:, 64 * c:64 * c + 64], T.pq[:, V * ph + 128 * c:V * ph + 128 * c + 128], T.pick[:], True, True, 128, 64) for c in range(4)],
           pqk[ph] + ["pick", b], [], pr)
        scan(T.t0[:, 256 * ph:256 * ph + 256], T.r0[:], B(b)[:, 0:256], A.min, A.max, 256, ["r0"], [b, ("t0", ph)], pr)
        mm([(cols(b2, 0, 128, 0, 32), T.t0[:, 256 * ph + 7:256 * ph + 256:8], T.ident[:], True, True, 32, 128)], [("t0", ph), "ident", b2], [], pr)
        ev("dve", H[ph][0:32, :], cols(b2, 0, 128, 0, 32), 128, [], [b2, ("h", ph, 0)], pr, 1.0, 1.0)
        mm([(cols(b3, 128 * c, 128), T.sel[0:32, 128 * c:128 * c + 128], H[ph][0:32, :], True, True, 128, 128) for c in range(4)],
           [("h", ph, 0), "selt", b3], [], pr + 1)
        ev("act", T.top[:, V * ph:V * ph + V], cols(b3, 0, V), V, ["col"], [b3, ("top", ph)], pr + 1, col(8), col(9))
    ac(T.e16[:], Z[:, 0:8], F.Identity, 8, ["zero", "col"], ["e16"], -235, bias=col(15))
    build(0, [W[0][:, EW:OB]], T.e16[:], None, ["e16"], [("wE", 0)], -234, "act", 8)
    build(1, [W[t][:, EW:OB] for t in range(1, RO)], T.e16[:], None, ["e16"], [("wE", t) for t in range(1, RO)], -233, "act", 8)
    ac(T.out0[:], T.pi[:], F.Identity, 1024, [("pi", x) for x in range(4)], ["out0"], -97)
    op("sync", lambda: Yq.dma_start(T.yp[:], T.out0[:]), 60, ["out0"], ["yp0"], -4, 3000, ("o0", 16, True))
    for x, q in enumerate(others):
        for a, n, e in ((0, V, ("act", "dve")[x]),) if x < 2 else ((0, 256, "act"), (256, 256, "dve")):
            c0 = V * q + a
            build(0, [W[0][:, OB + c0:OB + c0 + n]], T.land[:, c0:c0 + n], None, [("arr", 0)], [("wq", 0, x + a // 256)], -20 + x, e, n)

    def wkeys(t, full):
        return [("wq", t, x) for x in range(NR)] + [("w", t, 0), ("wE", t)] + ([("w", t, 1)] if full else [])

    def lists(t, s, row, phs, prio):
        b, c0, n = bank("*"), 32 * phs[0], 32 * len(phs)
        mm([(cols(b, 0, n), T.am[:, 144 * row + 15 - r:144 * row + 143 - r], T.xl[:, 1024 * t + 16 * c0 + r:1024 * t + 16 * (c0 + n):16],
             r == 0, r == 15, 128, n) for r in range(16)], [("xl", t, p) for p in phs] + [("am", row), b], [], prio)
        ac(T.eo[:, phs[0]:phs[-1] + 1, 32 * s:32 * s + 32], cols(b, 0, n), F.Relu, n, [], [b] + [("eo", s, p) for p in phs], prio, bias=8.0)

    def leave(t, ph, po):
        lo, hi = (0, 96) if t < RO - 1 else (96, 128)
        b = bank("*")
        grp = []
        for x in range(lo, hi, 32):
            grp.append((cols(b, 0, 128, x, x + 32), T.aa[:, 128 * ph + x:128 * ph + x + 32], T.ident[:], True, x > 0, 32, 128))
            if x == 0:
                grp.append((cols(b, 0, 128, 0, 32), T.u[:, 128 * ph:128 * ph + 32], T.nid[:], False, True, 32, 128))
        mm(grp, [("aa", 2 * y + ph) for y in range(lo // 32, hi // 32)] + [("u", ph), "ident", "nid", b], [], po)
        ac(T.go[lo:hi, 128 * ph:128 * ph + 128], cols(b, 0, 128, lo, hi), F.Abs, 128, [], [b, ("go", t, ph)], po)
        for c in range(lo // 8, hi // 8):
            e, q = ("act", Cq) if lo and ph and c % 2 else ("sync", Yq)
            a = V * ph + 128 * (c % 4)
            op(e, lambda q=q, c=c, a=a: q.dma_start(T.yp[8 + c // 4::16, a:a + 128], T.go[8 * c:8 * c + 8, 128 * ph:128 * ph + 128]),
               PAR["dq"], [("go", t, ph), "yp0"], [("yp", ph, c)], po, 2000, ("outs", 16 * 8 * RO, True))

    def plain(eng, out, win, gs, r, w, prio):
        if eng == "a":
            ac(out, win, F.Identity, V, r, w, prio, GA, scale=gs)
        else:
            ts(out, win, gs, None, A.mult, None, V, r, w, prio, GA)

    def xpart(t, ph, c):
        w = 8 * NPS[ph] * XL[t]
        return XT[ph][:, XO[t] + w * c:XO[t] + w * c + w]

    def kept(t, ph, p0):
        n, kk, lt, NP = 2 * t + ph, 32 * t + 32, XL[t], NPS[ph]
        m = -(-32 // min(8, 512 // (NP * lt)))
        cuts = [32 * x // m for x in range(m + 1)]
        for c in range(m):
            d = bank("d")
            a, b = cuts[c], cuts[c + 1]
            xw = (b - a) * NP * lt
            xs, ro, pr = XT[ph][:, XO[t] + a * NP * lt:XO[t] + b * NP * lt], RS[ph][:, a * NP * lt:b * NP * lt], p0 + .1 * c
            xk = [("xt", t if t > 1 else 0, ph, x) for x in range(a // 8, (b + 7) // 8)]
            mm([(B(d)[:, 0:xw], T.nkd[:], xs, True, False, 128, xw),
                (B(d)[:, 0:xw], H[ph][0:kk, :], T.seld[0:kk, a:b, 0:NP * lt], False, True, 128, xw)],
               xk + ["nkd", d] + [("seld", x) for x in range(a // 8, (b + 7) // 8)] + hk(ph, t), [], pr)
            if c < PAR["ob"][n]:
                db = T.db[:, 512 * (c % 2):512 * (c % 2) + xw]
                ac(db, B(d)[:, 0:xw], F.Identity, xw, [], [d, ("db", c % 2)], pr)
                scan(ro, db, xs, A.min, A.max, xw / 2, xk + [("db", c % 2), ("ro", ph)], [("ro", n, c)], pr)
            else:
                scan(ro, B(d)[:, 0:xw], xs, A.min, A.max, xw, xk + [("ro", ph)], [d, ("ro", n, c)], pr)
        scan(T.sr[:, GW * n:GW * n + 32 * NP], T["rs%d" % NP][:, 0:32 * NP], RS[ph][:, lt - 1:32 * NP * lt:lt], A.max, A.min, 16 * NP,
             [("rs", NP)], [("ro", ph), ("sr", n)], p0 + .4)

    for t in range(RO):
        gs = col(11 if t else 10)
        fk = wkeys(t, True) + ["lo", "col"]
        if t == 0:
            for ph in range(2):
                plain("ad"[ph], T.xl[:, V * ph:V * ph + V], W[0][:].indirect(T.lo[:, 32 * ph:32 * ph + 32]), gs, fk, [("xl", 0, ph)], -3)
            for s in range(8):
                lists(0, s, s, [0, 1], -2 + .1 * s)
        for ph in range(2):
            n = 2 * t + ph
            kk, NP = 32 * t + 32, NPS[ph]
            for s in PAR["rd"][n]:
                ts(RAW[ph][:, V * s:V * s + V], W[t][:, EW:WW].indirect(T.eo[:, ph, 32 * s:32 * s + 32]), gs, 0.0 if t else 1.0, A.mult, A.add, V,
                   wkeys(t, False) + [("eo", s, ph), "col"], [("raw", ph, s)], n - .4, GA)
            for grp in PAR["rg"][ph]:
                grp = [s for s in grp if s not in PAR["rd"][n]]
                if not grp:
                    continue
                a, b = grp[0], grp[-1] + 1
                ac(RAW[ph][:, V * a:V * b], W[t][:, EW:WW].indirect(T.eo[:, ph, 32 * a:32 * b]), F.Identity, V * (b - a),
                   wkeys(t, False) + [("eo", s, ph) for s in grp] + ["col"], [("raw", ph, s) for s in grp], n - .5 + .02 * a, GA,
                   scale=gs, bias=0.0 if t else 1.0)
            rk = [("raw", ph, s) for s in range(NP)] + ["pick"]

            def piece(k, c):
                return RAW[ph][:, V * k + 128 * c:V * k + 128 * c + 128]

            gt, sr = T.gt[:, GW * n:GW * n + 32 * NP], T.sr[:, GW * n + NP - 1:GW * n + 32 * NP:NP]
            if t == 0:
                for c in range(4):
                    b = bank()
                    mm([(B(b)[:, :, 9 * k:9 * k + 9], piece(k, c), T.pick9[:], True, True, 128, 72) for k in range(NP)], rk + ["pick9", b], [], n + .2 + .05 * c)
                    ev(PAR["x0"][c], xpart(0, ph, c), B(b)[:, :, 0:NP * 9], 72 * NP, [], [b, ("xt", 0, ph, c)], n + .2 + .05 * c)
                    copy(XM[ph][:, 8 * NP * c:8 * NP * (c + 1), 2:L], xpart(0, ph, c), [("xt", 0, ph, c)], [("xm", ph, c)], n + 1.5, 72 * NP)
                kept(0, ph, n + .3)
            else:
                b, b2 = bank(), bank()
                mm([(B(b)[:, c, k:8 * NP:NP], piece(k, c), T.pick[:, 7::8], True, True, 128, 8) for k in range(NP) for c in range(4)],
                   rk + [b], [], n + .1)
                ac(gt, B(b)[:, 0:4, 0:8 * NP], F.Identity, 32 * NP, [], [b, ("gt", n)], n + .1)
                mm([(B(b2)[:, 0:4, 0:8 * NP], T.nkd[:], gt, True, False, 128, 32 * NP),
                    (B(b2)[:, 0:4, 0:8 * NP], H[ph][0:kk, :], T.seld[0:kk, :, 0:NP], False, True, 128, 32 * NP)],
                   [("gt", n), "nkd", b2] + hk(ph, t), [], n + .2)
                zb = T.zb[:, GW * ph:GW * ph + 32 * NP]
                tt(zb, B(b2)[:, 0:4, 0:8 * NP], gt, A.max, 32 * NP, [("gt", n)], [b2, ("zb", ph)], n + .2)
                scan(T.zs[:, GW * n:GW * n + 32 * NP], T["rs%d" % NP][:, 0:32 * NP], zb, A.max, A.min, 32 * NP, [("zb", ph), ("rs", NP)], [("zs", n)], n + .2)
                tt(T.a1[:, 32 * n:32 * n + 32], T.zs[:, GW * n + NP - 1:GW * n + 32 * NP:NP], sr, A.min, 64, [("zs", n), ("sr", n)], [("a1", n)], n + .3)
                if t < RO - 1:
                    copy(XM[ph][:, 0:32 * NP, 3 - t], gt, [("gt", n)], [("xm", ph, c) for c in range(4)], n + .4, 32 * NP)
                    for c in range(4):
                        copy(xpart(t + 1, ph, c), XM[ph][:, 8 * NP * c:8 * NP * (c + 1), 2 - t:L], [("xm", ph, c)], [("xt", t + 1, ph, c)],
                             n + .5, 8 * NP * XL[t + 1])
                a = 1024 * t + V * ph
                plain(PAR["lde"][n], T.xl[:, a:a + V], W[t][:].indirect(T.lo[:, 32 * ph:32 * ph + 32]), gs, fk, [("xl", t, ph)], n - .3)
                lists(t, 7 + t, 0, [ph], n - .3)
            if ph == 0:
                P, pr, b, b2 = 8 if t == 0 else 1, n - .2, bank(), bank("*")
                z0 = 0 if t == 0 else 224 + 32 * t
                plain(PAR["xse"][t], T.xx[:, V * t:V * t + V], W[t][:].indirect(T.lo[:, 128:160]), gs, fk, [("xx", t)], pr)
                mm([(B(b)[:, 0:4, 0:8 * P], T.ident[:], T.own[:, ::8 // P], True, False, 128, 32 * P)] +
                   [(B(b)[:, c, 0:8 * P], T.xx[:, V * t + 128 * c:V * t + 128 * c + 128], T.pick[:, 8 // P - 1::8 // P], False, c == 3, 128, 8 * P)
                    for c in range(4)], [("xx", t), "own", "ident", "pick", b], [], pr)
                ac(T.ab[:, 0:32 * P], B(b)[:, 0:4, 0:8 * P], F.Abs, 32 * P, ["ownf"], [b, "ab"], pr, bias=T.ownf[:, 0:1])
                ac(T.zx[:, z0:z0 + 32 * P], T.ab[:, 0:32 * P], F.Relu, 32 * P, ["ab"], [("zx", t)], pr, bias=4096.0, scale=-4096.0)
                grp = [(cols(b2, 0, 32), T.nid[:], T.zx[:, z0 + p:z0 + 32 * P:P], p == 0, t == 0 and p == P - 1, 128, 32) for p in range(P)]
                if t:
                    grp.append((cols(b2, 0, 32), T.ident[:], T.pen[:, 4 * t - 4:4 * t, 0:8], False, True, 128, 32))
                mm(grp, [("zx", t), ("pen", t - 1), "ident", "nid", b2], [], pr)
                ac(T.pen[:, 4 * t:4 * t + 4, 0:8], cols(b2, 0, 32), F.Relu, 32, [], [b2, ("pen", t)], pr, bias=0.0 if t else 4096.0)
            if ph == 1 and t < RO - 1:
                for x, q in enumerate(others):
                    a = 512 * t + 128 * q
                    build(t + 1, [W[t + 1][:, OB + V * q:OB + V * q + V]], T.land[:, V * q:V * q + V], T.hl[0:kk + 32, a:a + 128],
                          [("arr", t + 1), ("arr", 0)], [("wq", t + 1, x)], n - .1, PAR["rem"][t][x])
            if t == RO - 1:
                leave(t - 1, ph, n + .5)
            places = ["cp", "ys"] if ph == 0 else ["cp"]
            order = places + list(range(NP, 8)) if t == 0 else list(range(NP, 7 + t)) + places + [7 + t]
            E = len(order)
            Q = "q%d" % ph
            for i, s in enumerate(order):
                pr = n + i / 10.0 - (.6 if t == 0 and ph == 0 and i < 2 else 0)
                mi = cnt["m"] % NM
                cnt["m"] += 1
                if s == "cp":
                    win, off, rk = W[t][:], T.lo[:, 64 + 32 * ph:96 + 32 * ph], wkeys(t, True) + ["lo"]
                elif s == "ys":
                    win, off, rk = W[t][:], T.lo[:, 160:192], wkeys(t, True) + ["lo"]
                else:
                    win, off, rk = W[t][:, EW:WW], T.eo[:, ph, 32 * s:32 * s + 32], wkeys(t, False) + [("eo", s, ph)]
                tt(T.m[:, V * mi:V * mi + V], win.indirect(off), T.top[:, V * ph:V * ph + V], A.max, V,
                   rk + [("top", ph)] + [("top", n, r) for r in range(15)], [("m", mi)], pr, GA)
                grp = []
                for c in range(4):
                    o = T[Q][:, 2 * c:2 * c + 2, i:8 * E:E]
                    if s == "ys":
                        grp.append((o, T.ident[:], T.pen[:, 4 * t + c, :], True, False, 16, 16))
                    grp.append((o, T.m[:, V * mi + 128 * c:V * mi + 128 * c + 128], T.sp[:, 16 * t:16 * t + 16], s != "ys", True, 128, 16))
                mm(grp, [("m", mi), ("sp", t, 0), ("sp", t, 1), Q] + ([("pen", t), "ident"] if s == "ys" else []), [], pr, 4)
            pr = n + .9
            hb, rr, a0 = T.hb[:, 256 * ph:256 * ph + 32 * E], T.rr[:, 256 * ph:256 * ph + 32 * E], 128 * ph + 32 * t
            aa, un = T.aa[:, a0:a0 + 32], T.u[:, a0:a0 + 32]
            ts(hb, T[Q][:, 1::2, 0:8 * E], MAGIC, MAGIC, A.add, A.subtract, 32 * E, [], [Q, ("topw", ph), ("hb", ph)], pr)
            tt(rr, T[Q][:, 0::2, 0:8 * E], hb, A.subtract, 32 * E, [("hb", ph)], [Q, ("rr", ph)], pr)
            scan(T.so[:, 256 * n:256 * n + 32 * E], T["rs%d" % E][:, 0:32 * E], rr, A.max, A.min, 16 * E, [("rs", E), ("rr", ph)], [("so", n)], pr)
            tt(aa, T.so[:, 256 * n + E - 1:256 * n + 32 * E:E], T.a1[:, 32 * n:32 * n + 32] if t else sr, A.min, 64,
               [("so", n), ("a1" if t else "sr", n)], [("aa", n)], pr)
            j = t + 1
            if t == RO - 1:
                leave(t, ph, pr)
                continue
            ac(un, aa, F.Relu, 32, [("aa", n)], [("u", n)], pr, bias=-2047.0 * (8 if t else 4608), scale=8.0 if t else 4608.0)
            b = bank("*")
            pd = cols(b, 0, 128, 32 * j, 32 * j + 32)
            mm([(pd, T.sel[0:kk, SN:SW], H[ph][0:kk, :], True, False, 32, 128), (pd, aa, T.ident[:], False, False, 32, 128),
                (pd, un, T.nid[:], False, True, 32, 128)], [("aa", n), ("u", n), "ident", "nid", b] + hk(ph, t), [], pr)
            ac(H[ph][32 * j:32 * j + 32, :], pd, F.Relu, 128, [], [b, ("h", ph, j)], pr, bias=1.0)
            if ph == 0:
                a = 512 * t + 128 * rank
                send(j, T.h0[:], T.hl[:, a:a + 128], [("h", 0, x) for x in range(4)], pr, PAR["lat"])
            build(j, [wblock(j, ph)], T.pq[:, V * ph:V * ph + V], H[ph][0:32 * j + 32, :], [("h", ph, x) for x in range(j + 1)] + pqk[ph],
                  [("w", j, ph)], pr + .01, dict(a="act", d="dve")[PAR["wown"][n]])
            c0, rows = (own0, 0)[ph], list(range(8)) + GAINED[j]
            for r in rows:
                op("sync", lambda r=r, j=j, ph=ph, c0=c0: Yq.dma_start(T.top[r::16, V * ph:V * ph + V], W[j][15::16, c0:c0 + V]), PAR["dq"],
                   [("w", j, ph), ("topw", ph)], [("top", 2 * j + ph, r)], pr, PAR["dlat"], ("tp%d" % (2 * j + ph), 16 * len(rows), True))
            kept(j, ph, pr + .5)
    return ops


def place(case, before, seq, back):
    hop = PAR["hop"]
    busy = dict(dve=[], act=[], pe=[], pool=[], sync=[])
    end = [0.0] * len(seq)
    for i in seq:
        e, _, cost, lat = case[i]
        if back:
            t0 = max([end[d] for d in before[i]] + [0.0]) + lat + hop
        else:
            t0 = max([end[d] + case[d][3] + hop for d in before[i]] + [0.0])
        lst = busy[e]
        x = len(lst)
        while x and lst[x - 1][1] > t0:
            x -= 1
        while x < len(lst) and lst[x][0] < t0 + cost:
            t0 = max(t0, lst[x][1])
            x += 1
        lst.insert(x, (t0, t0 + cost))
        end[i] = t0 + cost
    return end


def schedule(case, users, key, rnd, noise):
    n = len(case)
    deps = [c[1] for c in case]
    key = [x + noise * rnd() for x in key]
    for i in range(n):
        for d in deps[i]:
            key[i] = max(key[i], key[d] + 1e-3)
    seq = sorted(range(n), key=lambda i: key[i])
    for _ in range(2):
        end = place(case, deps, seq, False)
        end = place(case, users, sorted(range(n), key=lambda i: -end[i]), True)
        seq = sorted(range(n), key=lambda i: -end[i])
    end = place(case, deps, seq, False)
    return max(end), [end[i] - case[i][2] for i in range(n)]


def span(case, order):
    hop = PAR["hop"]
    free = dict(dve=0.0, act=0.0, pe=0.0, pool=0.0, sync=0.0)
    done = [0.0] * len(order)
    for i in order:
        e, deps, cost, lat = case[i]
        t0 = max([free[e]] + [done[d] for d in deps])
        free[e] = t0 + cost
        done[i] = t0 + cost + lat + hop
    return max(done)


def anneal(case, start0, marks, rnd, moves, hot):
    names = ["dve", "act", "pe", "pool", "sync"]
    eng = [names.index(c[0]) for c in case]
    deps = [list(c[1]) for c in case]
    cost = [c[2] for c in case]
    lat = [c[3] + PAR["hop"] for c in case]
    n, amp = len(case), PAR["amp"]

    def decode(seq, p0, p1, start, done, S, Z):
        dirty = -1.0
        for p in range(p0, n):
            i = seq[p]
            old = start[i]
            if p >= p1 and old > dirty:
                return p
            t0 = 0.0
            for d in deps[i]:
                if done[d] > t0:
                    t0 = done[d]
            s, z, c = S[eng[i]], Z[eng[i]], cost[i]
            if not z or z[-1] <= t0:
                s.append(t0)
                z.append(t0 + c)
            else:
                m = x = len(z)
                while x and z[x - 1] > t0:
                    x -= 1
                while x < m and s[x] < t0 + c:
                    t0 = z[x]
                    x += 1
                s.insert(x, t0)
                z.insert(x, t0 + c)
            if t0 != old:
                old = (t0 if t0 > old else old) + c + lat[i] + 1.0
                if old > dirty:
                    dirty = old
                start[i] = t0
                done[i] = t0 + c + lat[i]
        return n

    def value(done):
        v = max(done)
        for i, w in marks:
            v += w * done[i]
        return v

    def counts(seq):
        c, out = [0] * 5, []
        for i in seq:
            out.append(tuple(c))
            c[eng[i]] += 1
        return out + [tuple(c)]

    seq = sorted(range(n), key=lambda i: start0[i])
    start, done = [-1.0] * n, [0.0] * n
    S, Z = [[] for _ in names], [[] for _ in names]
    decode(seq, 0, n, start, done, S, Z)
    val = value(done)
    seq.sort(key=lambda i: start[i])
    pre = counts(seq)
    best = (val, seq, start)
    for it in range(moves):
        p = int(rnd() * n)
        i, step = seq[p], amp * rnd() ** 2
        if rnd() < 0.5:
            lim, b = start[i] + step, p + 1
            while b < n and start[seq[b]] < lim:
                b += 1
            take, front, back = {i}, [], [i]
            for j in seq[p + 1:b]:
                for d in deps[j]:
                    if d in take:
                        take.add(j)
                        back.append(j)
                        break
                else:
                    front.append(j)
            if not front:
                continue
            new, p0, p1 = seq[:p] + front + back + seq[b:], p, b
        else:
            lim, a = start[i] - step, p
            while a > 0 and start[seq[a - 1]] > lim:
                a -= 1
            need, front, back = set(deps[i]), [i], []
            for j in reversed(seq[a:p]):
                if j in need:
                    need.update(deps[j])
                    front.append(j)
                else:
                    back.append(j)
            if not back:
                continue
            new, p0, p1 = seq[:a] + front[::-1] + back[::-1] + seq[p + 1:], a, p + 1
        left = pre[p0]
        S2, Z2 = [S[e][:left[e]] for e in range(5)], [Z[e][:left[e]] for e in range(5)]
        st2, dn2 = list(start), list(done)
        p = decode(new, p0, p1, st2, dn2, S2, Z2)
        v = value(dn2)
        if v <= val or rnd() < math.exp((val - v) / (hot * (PAR["cold"] / hot) ** (it / moves))):
            left = pre[p]
            val, start, done = v, st2, dn2
            S, Z = [S2[e] + S[e][left[e]:] for e in range(5)], [Z2[e] + Z[e][left[e]:] for e in range(5)]
            seq = sorted(new, key=lambda i: st2[i])
            pre = counts(seq)
            if v < best[0]:
                best = (v, seq, start)
    return best[1], list(best[2]), best[0]


def choose(g, core, T, topo, rank):
    if "order" not in KEPT:
        seed = [12345]

        def rnd():
            seed[0] = (seed[0] * 1103515245 + 12345) % 2147483648
            return seed[0] / 2147483648.0

        ops = plan(g, core, T, topo, rank)
        n = len(ops)
        free = [(o["eng"], tuple(o["deps"] | o["soft"]), o["cost"], o["lat"]) for o in ops]
        users = [[] for _ in ops]
        first, last = {}, {}
        for i, o in enumerate(ops):
            for d in free[i][1]:
                users[d].append(i)
            for b in o["r"] + o["w"]:
                if b in KEPT["kind"]:
                    (first if o["eng"] == "pe" else last).setdefault(b, []).append(i)
        marks = [(i, PAR["marks"][o["w"][-1][0]]) for i, o in enumerate(ops)
                 if o["w"] and o["w"][-1] not in KEPT["kind"] and o["w"][-1][0] in PAR["marks"]]

        def banks(start):
            bank, more, held = {}, {}, {}
            for b in sorted(first, key=lambda b: min(start[i] for i in first[b])):
                names = dict(g=GB, d=DB)[KEPT["kind"][b]] if KEPT["kind"][b] != "*" else GB + DB
                t0 = min(start[i] for i in first[b])
                x = min(names, key=lambda x: (max(held.get(x, (0, 0))[0], t0 - 300), rnd()))
                for i in first[b]:
                    more[i] = tuple(last[held[x][1]]) if x in held else ()
                bank[b], held[x] = x, (max(start[i] + free[i][2] for i in last[b]), b)
            case = [(c[0], c[1] + more.get(i, ()), c[2], c[3]) for i, c in enumerate(free)]
            moved = True
            while moved:
                moved = False
                for i in range(n):
                    for d in case[i][1]:
                        if start[i] <= start[d]:
                            start[i], moved = start[d] + 1e-3, True
            return bank, more, case

        def improve(start, steps, keep):
            for moves, hot, weight in steps:
                bank, more, case = banks(start)
                order, start, val = anneal(case, start, [(i, w * weight) for i, w in marks], rnd, moves, hot)
                val = span(case, order)
                if keep is None or val < keep[0]:
                    keep = (val, order, bank, more, case, list(start))
            return keep

        keep = None
        for s in range(PAR["starts"]):
            best = (1e18, [max(o["prio"], -3) * 8000 + o["prio"] for o in ops])
            for k in range(PAR["tries"]):
                best = min(best, schedule(free, users, best[1], rnd, PAR["noise"] * rnd()))
            keep = improve(anneal(free, best[1], marks, rnd, PAR["first"], 200.0)[1], PAR["steps"], keep)
        keep = improve(list(keep[5]), PAR["more"], keep)
        KEPT.update(order=keep[1], bank=keep[2], more=keep[3], cases=[keep[4]])
    ops = plan(g, core, T, topo, rank)
    for i, d in KEPT["more"].items():
        ops[i]["deps"] |= set(d)
    return ops, KEPT["order"]


def rank_program(g, core, T, topo):
    rank = T.rank_of(core)
    if rank is None:
        return
    S = T.sem
    ops, order = choose(g, core, T, topo, rank)
    queue = dict(dve=g.vector, act=g.scalar, pe=g.tensor, pool=g, sync=g.sync)
    needed = set(d for o in ops for d in o["deps"] if not (o["eng"] == "pe" and ops[d]["eng"] == "pe"))
    count, token, seen = {}, {}, {}
    for i in order:
        o = ops[i]
        e = o["eng"]
        want = {}
        for d in o["deps"]:
            if e == "pe" and ops[d]["eng"] == "pe":
                continue
            sem = ops[d]["sem"]
            s, v = sem[3:] if d in o["war"] and sem is not None and not sem[2] else token[d]
            want[s] = max(want.get(s, 0), v)
        for s in sorted(want):
            if seen.get((e, s), 0) < want[s]:
                queue[e].wait_ge(S[s], want[s])
                seen[(e, s)] = want[s]
        ins = o["fn"]()
        if o["sem"] is not None:
            if o["sem"][2]:
                ins.then_inc(S[o["sem"][0]], 16)
            token[i] = o["sem"][:2]
        elif i in needed:
            count[e] = count.get(e, 0) + 1
            ins.then_inc(S[e], 1)
            token[i] = (e, count[e])
    g.sync.wait_ge(S.outs, 16 * 8 * RO)
    for o in ops:
        if o["sem"] is not None and not o["sem"][2]:
            g.wait_ge(S[o["sem"][3]], o["sem"][4])
